import numpy as np
import ml_dtypes


def mxq(x, axis, fmt="e4m3"):
    dtype, down = {"e4m3": (ml_dtypes.float8_e4m3fn, 7), "e5m2": (ml_dtypes.float8_e5m2, 14)}[fmt]
    v = np.moveaxis(np.asarray(x, np.float32).astype(ml_dtypes.bfloat16).astype(np.float64), axis, -1)
    blocks = v.reshape(v.shape[:-1] + (-1, 32))
    amax = np.abs(blocks).max(-1, keepdims=True)
    byte = np.maximum(np.where(amax > 0, np.frexp(amax)[1] - 1 + 127, 0) - down, 1)
    scale = np.exp2(byte - 127.0)
    codes = (blocks / scale).astype(np.float32).astype(dtype).astype(np.float64)
    return np.moveaxis((codes * scale).reshape(v.shape), -1, axis)


WIDE = False


def mx_kscale(k):
    if not WIDE:
        return np.ones(k)
    levels = np.array([10, -10, 5, -5, 0])
    if k % 512:
        return np.exp2(np.random.permutation(np.resize(levels, k // 32))).repeat(32)
    a = np.empty((k // 512, 16))
    for p in range(k // 512):
        a[p, :8] = np.random.permutation(np.resize(levels, 8))
        for g in range(8):
            far = levels[np.abs(levels - a[p, g]) >= 10]
            a[p, g + 8] = far[np.random.randint(len(far))]
    return np.exp2(a.ravel()).repeat(32)


def f64(x):
    return np.asarray(x).astype(np.float64)


def striped(idx):
    return np.tile(idx.reshape(-1, 16).T, (8, 1)).astype(np.uint16)


def unstriped(offs):
    return offs[:16].T.reshape(-1).astype(np.int64)


def pack_weight(w):
    k, n = w.shape
    w = f64(np.asarray(w, np.float32).astype(ml_dtypes.bfloat16)).reshape(k // 32, 32, n)
    amax = np.abs(w).max(1)
    byte = np.clip(np.where(amax > 0, np.frexp(amax)[1] - 1 + 127 - 7, 1), 1, 254)
    scaled = (w * np.exp2(127.0 - byte)[:, None, :]).reshape(k, n).astype(np.float32)
    words = np.ascontiguousarray(scaled.reshape(k // 512, 128, 4, n).transpose(0, 1, 3, 2)).astype(ml_dtypes.float8_e4m3fn).view(np.uint8)
    return words, np.ascontiguousarray(byte.astype(np.uint8).reshape(k // 512, 16, n))


def unpack_weight(words, scales):
    g, p, n, _ = words.shape
    vals = np.ascontiguousarray(words).view(ml_dtypes.float8_e4m3fn).astype(np.float64) * np.repeat(np.exp2(scales.astype(np.float64) - 127.0), 8, axis=1)[..., None]
    return vals.transpose(0, 1, 3, 2).reshape(g * 512, n)


K, T, D, S, V, N = 1024, 2048, 8, 2048, 256, 256


def setup_inputs():
    n = np.random.standard_normal
    s = mx_kscale(K)[:, None]
    words, scales = pack_weight(n((K, N)) / np.sqrt(K) / s)
    return {
        "xT": (n((K, T)) * s).astype(np.float32),
        "w_words": words,
        "w_scales": scales,
        "b": (0.3 * n((N, 1))).astype(np.float32),
        "offs": striped(np.concatenate([np.random.permutation(T)[:V] for _ in range(D)])),
    }


def reference(xT, w_words, w_scales, b, offs):
    w = unpack_weight(w_words, w_scales)
    idx = unstriped(offs)
    x = np.empty((K, V))
    for l in range(D):
        r = l // 4 * (4 * K // D) + l % 4 + 4 * np.arange(K // D)
        x[r] = f64(xT)[r][:, idx[l * V:(l + 1) * V]]
    xq = mxq(x, 0, "e4m3")
    return (w.T @ xq) + f64(b)

@@ -1,0 +1,99 @@
+from contextlib import ExitStack
+
+import concourse.mybir as mybir
+
+K, T, D, V, N = 1024, 2048, 8, 256, 256
+FLOPS = 2 * K * V * N
+
+F32 = mybir.dt.float32
+BF16 = mybir.dt.bfloat16
+I32 = mybir.dt.int32
+U32 = mybir.dt.uint32
+U16 = mybir.dt.uint16
+U8 = mybir.dt.uint8
+FP8X4 = mybir.dt.float8_e4m3fn_x4
+IDENTITY = mybir.ActivationFunctionType.Identity
+
+P = 128
+PACK = 4
+K_PASS = P * PACK
+PASSES = K // K_PASS
+M_TILES = N // P
+LIST_COLS = V // 16
+LOADS = ((0, 4), (4, 2), (6, 1), (7, 1))
+
+
+def tile_picked_grid_lin_bias_sub_l_kernel(tc, xT, w_words, w_scales, b, offs, out):
+    nc = tc.nc
+    with ExitStack() as ctx:
+        keep = ctx.enter_context(tc.tile_pool(name="keep", bufs=1))
+        psum = ctx.enter_context(tc.psum_pool(name="psum", bufs=1))
+
+        offsets = keep.tile([P, D * LIST_COLS], U16, name="offsets")
+        w_codes = keep.tile([P, PASSES, N], U32, name="w_codes", align_bytes=64)
+        w_plane = keep.tile([P, PASSES, N], U8, name="w_plane", align_bytes=64)
+        bias = keep.tile([P, M_TILES, 8], F32, name="bias")
+        warm_in = keep.tile([P, 1], F32, name="warm_in")
+        warm_out = keep.tile([P, 1], F32, name="warm_out")
+
+        nc.vector.memset(w_plane[:].rearrange("p a m -> p (a m)").bitcast(I32), 0)
+        nc.vector.memset(warm_in[:], 0.0)
+        nc.scalar.activation(warm_out[:], warm_in[:], IDENTITY, bias=warm_in[:])
+
+        windows = []
+        for first, count in LOADS:
+            a, t = divmod(first, PACK)
+            rows = xT[a * K_PASS : (a + 1) * K_PASS, :].rearrange("(p t) c -> p (t c)", t=PACK)
+            tables = keep.tile([P, count * T], F32, name="tables%d" % first)
+            nc.sync.dma_start(tables[:], rows[:, t * T : (t + count) * T])
+            if first == 0:
+                nc.sync.dma_start(offsets[:], offs)
+            windows.extend(tables[:, j * T : (j + 1) * T] for j in range(count))
+
+        for q in range(4):
+            nc.sync.dma_start(
+                w_plane[32 * q : 32 * q + 4, :, :].bitcast(I32),
+                w_scales[:, 4 * q : 4 * q + 4, :].rearrange("a r m -> r a m").bitcast(I32),
+            )
+        nc.sync.dma_start(
+            w_codes[:].bitcast(I32),
+            w_words.rearrange("a p m r -> p a (m r)").bitcast(I32),
+        )
+        with nc.allow_non_contiguous_dma(reason="one bias value for each partition"):
+            nc.sync.dma_start(bias[:, :, 0:1], b.rearrange("(c p) o -> p c o", p=P))
+
+        x_codes = []
+        x_planes = []
+        for a in range(PASSES):
+            grouped = keep.tile([P, V, PACK], BF16, name="grouped%d" % a, align_bytes=64)
+            for t in range(PACK):
+                level = PACK * a + t
+                piece = offsets[:, level * LIST_COLS : (level + 1) * LIST_COLS]
+                nc.vector.tensor_copy(grouped[:, :, t], windows[level].indirect(piece))
+            codes = keep.tile([P, V], U32, name="x_codes%d" % a, align_bytes=64)
+            plane = keep.tile([P, V], U8, name="x_plane%d" % a, align_bytes=64)
+            nc.vector.quantize_mx(
+                out=codes[:].bitcast(FP8X4), scales=plane[:], in_=grouped[:].rearrange("p v t -> p (v t)")
+            )
+            x_codes.append(codes)
+            x_planes.append(plane)
+
+        sums = [psum.tile([P, V], F32, name="sums%d" % c) for c in range(M_TILES)]
+        for a in range(PASSES):
+            for c in range(M_TILES):
+                cols = slice(c * P, (c + 1) * P)
+                nc.tensor.matmul_mx(
+                    out=sums[c][:],
+                    lhsT=w_codes[:, a, cols].bitcast(FP8X4),
+                    lhsT_scale=w_plane[:, a, cols],
+                    rhs=x_codes[a][:].bitcast(FP8X4),
+                    rhs_scale=x_planes[a][:],
+                    start=(a == 0),
+                    stop=(a == PASSES - 1),
+                )
+
+        results = [keep.tile([P, V], F32, name="result%d" % c) for c in range(M_TILES)]
+        nc.scalar.activation(results[0][:], sums[0][:], IDENTITY, bias=bias[:, 0, 0:1])
+        nc.scalar.dma_start(out[0:P, :], results[0][:])
+        nc.vector.tensor_scalar_add(results[1][:], sums[1][:], bias[:, 1, 0:1])
+        nc.sync.dma_start(out[P : 2 * P, :], results[1][:])

@@ -20,6 +20,7 @@ K_PASS = P * PACK
 PASSES = K // K_PASS
 M_TILES = N // P
 LIST_COLS = V // 16
+HALF = V // 2
 LOADS = ((0, 4), (4, 2), (6, 1), (7, 1))
 
 
@@ -50,50 +51,51 @@ def tile_picked_grid_lin_bias_sub_l_kernel(tc, xT, w_words, w_scales, b, offs, o
                 nc.sync.dma_start(offsets[:], offs)
             windows.extend(tables[:, j * T : (j + 1) * T] for j in range(count))
 
+        words = w_words.rearrange("a p m r -> a p (m r)")
+        nc.sync.dma_start(w_codes[:, 0, :].bitcast(I32), words[0].bitcast(I32))
         for q in range(4):
             nc.sync.dma_start(
                 w_plane[32 * q : 32 * q + 4, :, :].bitcast(I32),
                 w_scales[:, 4 * q : 4 * q + 4, :].rearrange("a r m -> r a m").bitcast(I32),
             )
-        nc.sync.dma_start(
-            w_codes[:].bitcast(I32),
-            w_words.rearrange("a p m r -> p a (m r)").bitcast(I32),
-        )
+        nc.sync.dma_start(w_codes[:, 1, :].bitcast(I32), words[1].bitcast(I32))
         with nc.allow_non_contiguous_dma(reason="one bias value for each partition"):
             nc.sync.dma_start(bias[:, :, 0:1], b.rearrange("(c p) o -> p c o", p=P))
 
-        x_codes = []
-        x_planes = []
+        halves = [slice(h * HALF, (h + 1) * HALF) for h in range(2)]
+        sums = [[psum.tile([P, HALF], F32, name="sums%d_%d" % (h, c)) for c in range(M_TILES)] for h in range(2)]
         for a in range(PASSES):
             grouped = keep.tile([P, V, PACK], BF16, name="grouped%d" % a, align_bytes=64)
             for t in range(PACK):
                 level = PACK * a + t
                 piece = offsets[:, level * LIST_COLS : (level + 1) * LIST_COLS]
                 nc.vector.tensor_copy(grouped[:, :, t], windows[level].indirect(piece))
-            codes = keep.tile([P, V], U32, name="x_codes%d" % a, align_bytes=64)
-            plane = keep.tile([P, V], U8, name="x_plane%d" % a, align_bytes=64)
-            nc.vector.quantize_mx(
-                out=codes[:].bitcast(FP8X4), scales=plane[:], in_=grouped[:].rearrange("p v t -> p (v t)")
-            )
-            x_codes.append(codes)
-            x_planes.append(plane)
-
-        sums = [psum.tile([P, V], F32, name="sums%d" % c) for c in range(M_TILES)]
-        for a in range(PASSES):
-            for c in range(M_TILES):
-                cols = slice(c * P, (c + 1) * P)
-                nc.tensor.matmul_mx(
-                    out=sums[c][:],
-                    lhsT=w_codes[:, a, cols].bitcast(FP8X4),
-                    lhsT_scale=w_plane[:, a, cols],
-                    rhs=x_codes[a][:].bitcast(FP8X4),
-                    rhs_scale=x_planes[a][:],
-                    start=(a == 0),
-                    stop=(a == PASSES - 1),
+            x_codes = keep.tile([P, V], U32, name="x_codes%d" % a, align_bytes=64)
+            x_plane = keep.tile([P, V], U8, name="x_plane%d" % a, align_bytes=64)
+            for points in halves:
+                nc.vector.quantize_mx(
+                    out=x_codes[:, points].bitcast(FP8X4),
+                    scales=x_plane[:, points],
+                    in_=grouped[:, points, :].rearrange("p v t -> p (v t)"),
                 )
+            for h, points in enumerate(halves):
+                for c in range(M_TILES):
+                    cols = slice(c * P, (c + 1) * P)
+                    nc.tensor.matmul_mx(
+                        out=sums[h][c][:],
+                        lhsT=w_codes[:, a, cols].bitcast(FP8X4),
+                        lhsT_scale=w_plane[:, a, cols],
+                        rhs=x_codes[:, points].bitcast(FP8X4),
+                        rhs_scale=x_plane[:, points],
+                        start=(a == 0),
+                        stop=(a == PASSES - 1),
+                    )
 
-        results = [keep.tile([P, V], F32, name="result%d" % c) for c in range(M_TILES)]
-        nc.scalar.activation(results[0][:], sums[0][:], IDENTITY, bias=bias[:, 0, 0:1])
-        nc.scalar.dma_start(out[0:P, :], results[0][:])
-        nc.vector.tensor_scalar_add(results[1][:], sums[1][:], bias[:, 1, 0:1])
-        nc.sync.dma_start(out[P : 2 * P, :], results[1][:])
+        out_view = out.rearrange("(c p) v -> p c v", p=P)
+        results = [keep.tile([P, M_TILES, HALF], F32, name="result%d" % h) for h in range(2)]
+        for h in range(2):
+            nc.scalar.activation(results[h][:, 0, :], sums[h][0][:], IDENTITY, bias=bias[:, 0, 0:1])
+            nc.vector.tensor_scalar_add(results[h][:, 1, :], sums[h][1][:], bias[:, 1, 0:1])
+        nc.sync.dma_start(out_view[:, :, halves[0]], results[0][:])
+        nc.scalar.dma_start(out_view[:, 0, halves[1]], results[1][:, 0, :])
+        nc.sync.dma_start(out_view[:, 1, halves[1]], results[1][:, 1, :])

@@ -78,8 +78,8 @@ def tile_picked_grid_lin_bias_sub_l_kernel(tc, xT, w_words, w_scales, b, offs, o
                     scales=x_plane[:, points],
                     in_=grouped[:, points, :].rearrange("p v t -> p (v t)"),
                 )
-            for h, points in enumerate(halves):
-                for c in range(M_TILES):
+            for c in range(M_TILES):
+                for h, points in enumerate(halves):
                     cols = slice(c * P, (c + 1) * P)
                     nc.tensor.matmul_mx(
                         out=sums[h][c][:],
@@ -91,11 +91,8 @@ def tile_picked_grid_lin_bias_sub_l_kernel(tc, xT, w_words, w_scales, b, offs, o
                         stop=(a == PASSES - 1),
                     )
 
-        out_view = out.rearrange("(c p) v -> p c v", p=P)
-        results = [keep.tile([P, M_TILES, HALF], F32, name="result%d" % h) for h in range(2)]
-        for h in range(2):
-            nc.scalar.activation(results[h][:, 0, :], sums[h][0][:], IDENTITY, bias=bias[:, 0, 0:1])
-            nc.vector.tensor_scalar_add(results[h][:, 1, :], sums[h][1][:], bias[:, 1, 0:1])
-        nc.sync.dma_start(out_view[:, :, halves[0]], results[0][:])
-        nc.scalar.dma_start(out_view[:, 0, halves[1]], results[1][:, 0, :])
-        nc.sync.dma_start(out_view[:, 1, halves[1]], results[1][:, 1, :])
+        for c in range(M_TILES):
+            result = keep.tile([P, V], F32, name="result%d" % c)
+            nc.scalar.activation(result[:, halves[0]], sums[0][c][:], IDENTITY, bias=bias[:, c, 0:1])
+            nc.vector.tensor_scalar_add(result[:, halves[1]], sums[1][c][:], bias[:, c, 0:1])
+            nc.sync.dma_start(out[c * P : (c + 1) * P, :], result[:])

@@ -21,7 +21,8 @@ PASSES = K // K_PASS
 M_TILES = N // P
 LIST_COLS = V // 16
 HALF = V // 2
-LOADS = ((0, 4), (4, 2), (6, 1), (7, 1))
+LOADS = ((0, 4), (4, 3), (7, 1))
+PAIRED = 2
 
 
 def tile_picked_grid_lin_bias_sub_l_kernel(tc, xT, w_words, w_scales, b, offs, out):
@@ -34,12 +35,8 @@ def tile_picked_grid_lin_bias_sub_l_kernel(tc, xT, w_words, w_scales, b, offs, o
         w_codes = keep.tile([P, PASSES, N], U32, name="w_codes", align_bytes=64)
         w_plane = keep.tile([P, PASSES, N], U8, name="w_plane", align_bytes=64)
         bias = keep.tile([P, M_TILES, 8], F32, name="bias")
-        warm_in = keep.tile([P, 1], F32, name="warm_in")
-        warm_out = keep.tile([P, 1], F32, name="warm_out")
 
         nc.vector.memset(w_plane[:].rearrange("p a m -> p (a m)").bitcast(I32), 0)
-        nc.vector.memset(warm_in[:], 0.0)
-        nc.scalar.activation(warm_out[:], warm_in[:], IDENTITY, bias=warm_in[:])
 
         windows = []
         for first, count in LOADS:
@@ -62,6 +59,7 @@ def tile_picked_grid_lin_bias_sub_l_kernel(tc, xT, w_words, w_scales, b, offs, o
         with nc.allow_non_contiguous_dma(reason="one bias value for each partition"):
             nc.sync.dma_start(bias[:, :, 0:1], b.rearrange("(c p) o -> p c o", p=P))
 
+        picked = keep.tile([P, PAIRED, V], F32, name="picked")
         halves = [slice(h * HALF, (h + 1) * HALF) for h in range(2)]
         sums = [[psum.tile([P, HALF], F32, name="sums%d_%d" % (h, c)) for c in range(M_TILES)] for h in range(2)]
         for a in range(PASSES):
@@ -69,7 +67,12 @@ def tile_picked_grid_lin_bias_sub_l_kernel(tc, xT, w_words, w_scales, b, offs, o
             for t in range(PACK):
                 level = PACK * a + t
                 piece = offsets[:, level * LIST_COLS : (level + 1) * LIST_COLS]
-                nc.vector.tensor_copy(grouped[:, :, t], windows[level].indirect(piece))
+                if a == PASSES - 1 and t < PAIRED:
+                    nc.vector.tensor_copy(picked[:, t, :], windows[level].indirect(piece))
+                    if t == PAIRED - 1:
+                        nc.scalar.activation(grouped[:, :, 0:PAIRED], picked[:].rearrange("p t v -> p v t"), IDENTITY)
+                else:
+                    nc.vector.tensor_copy(grouped[:, :, t], windows[level].indirect(piece))
             x_codes = keep.tile([P, V], U32, name="x_codes%d" % a, align_bytes=64)
             x_plane = keep.tile([P, V], U8, name="x_plane%d" % a, align_bytes=64)
             for points in halves:

@@ -21,7 +21,8 @@ PASSES = K // K_PASS
 M_TILES = N // P
 LIST_COLS = V // 16
 HALF = V // 2
-LOADS = ((0, 4), (4, 3), (7, 1))
+LOADS = ((0, 4), (4, 2), (6, 1), (7, 1))
+BLOCK = 32
 PAIRED = 2
 
 
@@ -34,9 +35,11 @@ def tile_picked_grid_lin_bias_sub_l_kernel(tc, xT, w_words, w_scales, b, offs, o
         offsets = keep.tile([P, D * LIST_COLS], U16, name="offsets")
         w_codes = keep.tile([P, PASSES, N], U32, name="w_codes", align_bytes=64)
         w_plane = keep.tile([P, PASSES, N], U8, name="w_plane", align_bytes=64)
-        bias = keep.tile([P, M_TILES, 8], F32, name="bias")
+        bias_rows = keep.tile([P, M_TILES, BLOCK], F32, name="bias_rows", align_bytes=64)
+        bias = keep.tile([P, M_TILES, BLOCK], F32, name="bias", align_bytes=64)
 
         nc.vector.memset(w_plane[:].rearrange("p a m -> p (a m)").bitcast(I32), 0)
+        nc.vector.memset(bias_rows[:], 0.0)
 
         windows = []
         for first, count in LOADS:
@@ -56,8 +59,7 @@ def tile_picked_grid_lin_bias_sub_l_kernel(tc, xT, w_words, w_scales, b, offs, o
                 w_scales[:, 4 * q : 4 * q + 4, :].rearrange("a r m -> r a m").bitcast(I32),
             )
         nc.sync.dma_start(w_codes[:, 1, :].bitcast(I32), words[1].bitcast(I32))
-        with nc.allow_non_contiguous_dma(reason="one bias value for each partition"):
-            nc.sync.dma_start(bias[:, :, 0:1], b.rearrange("(c p) o -> p c o", p=P))
+        nc.sync.dma_start(bias_rows[0:P:BLOCK, :, :], b.rearrange("(c q j) o -> q c (j o)", c=M_TILES, j=BLOCK))
 
         picked = keep.tile([P, PAIRED, V], F32, name="picked")
         halves = [slice(h * HALF, (h + 1) * HALF) for h in range(2)]
@@ -67,7 +69,7 @@ def tile_picked_grid_lin_bias_sub_l_kernel(tc, xT, w_words, w_scales, b, offs, o
             for t in range(PACK):
                 level = PACK * a + t
                 piece = offsets[:, level * LIST_COLS : (level + 1) * LIST_COLS]
-                if a == PASSES - 1 and t < PAIRED:
+                if a == 0 and t < PAIRED:
                     nc.vector.tensor_copy(picked[:, t, :], windows[level].indirect(piece))
                     if t == PAIRED - 1:
                         nc.scalar.activation(grouped[:, :, 0:PAIRED], picked[:].rearrange("p t v -> p v t"), IDENTITY)
@@ -94,6 +96,8 @@ def tile_picked_grid_lin_bias_sub_l_kernel(tc, xT, w_words, w_scales, b, offs, o
                         stop=(a == PASSES - 1),
                     )
 
+        for c in range(M_TILES):
+            nc.vector.transpose(bias[:, c, :], bias_rows[:, c, :])
         for c in range(M_TILES):
             result = keep.tile([P, V], F32, name="result%d" % c)
             nc.scalar.activation(result[:, halves[0]], sums[0][c][:], IDENTITY, bias=bias[:, c, 0:1])

@@ -41,14 +41,13 @@ def tile_picked_grid_lin_bias_sub_l_kernel(tc, xT, w_words, w_scales, b, offs, o
         nc.vector.memset(w_plane[:].rearrange("p a m -> p (a m)").bitcast(I32), 0)
         nc.vector.memset(bias_rows[:], 0.0)
 
+        nc.sync.dma_start(offsets[:], offs)
         windows = []
         for first, count in LOADS:
             a, t = divmod(first, PACK)
             rows = xT[a * K_PASS : (a + 1) * K_PASS, :].rearrange("(p t) c -> p (t c)", t=PACK)
             tables = keep.tile([P, count * T], F32, name="tables%d" % first)
             nc.sync.dma_start(tables[:], rows[:, t * T : (t + count) * T])
-            if first == 0:
-                nc.sync.dma_start(offsets[:], offs)
             windows.extend(tables[:, j * T : (j + 1) * T] for j in range(count))
 
         words = w_words.rearrange("a p m r -> a p (m r)")
@@ -100,6 +99,6 @@ def tile_picked_grid_lin_bias_sub_l_kernel(tc, xT, w_words, w_scales, b, offs, o
             nc.vector.transpose(bias[:, c, :], bias_rows[:, c, :])
         for c in range(M_TILES):
             result = keep.tile([P, V], F32, name="result%d" % c)
-            nc.scalar.activation(result[:, halves[0]], sums[0][c][:], IDENTITY, bias=bias[:, c, 0:1])
-            nc.vector.tensor_scalar_add(result[:, halves[1]], sums[1][c][:], bias[:, c, 0:1])
+            nc.scalar.activation(result[:, halves[1]], sums[1][c][:], IDENTITY, bias=bias[:, c, 0:1])
+            nc.vector.tensor_scalar_add(result[:, halves[0]], sums[0][c][:], bias[:, c, 0:1])
             nc.sync.dma_start(out[c * P : (c + 1) * P, :], result[:])

@@ -23,6 +23,7 @@ LIST_COLS = V // 16
 HALF = V // 2
 LOADS = ((0, 4), (4, 2), (6, 1), (7, 1))
 BLOCK = 32
+BURST = 256
 PAIRED = 2
 
 
@@ -32,9 +33,9 @@ def tile_picked_grid_lin_bias_sub_l_kernel(tc, xT, w_words, w_scales, b, offs, o
         keep = ctx.enter_context(tc.tile_pool(name="keep", bufs=1))
         psum = ctx.enter_context(tc.psum_pool(name="psum", bufs=1))
 
-        offsets = keep.tile([P, D * LIST_COLS], U16, name="offsets")
-        w_codes = keep.tile([P, PASSES, N], U32, name="w_codes", align_bytes=64)
-        w_plane = keep.tile([P, PASSES, N], U8, name="w_plane", align_bytes=64)
+        offsets = keep.tile([P, D * LIST_COLS], U16, name="offsets", align_bytes=BURST)
+        w_codes = keep.tile([P, PASSES, N], U32, name="w_codes", align_bytes=BURST)
+        w_plane = keep.tile([P, PASSES, N], U8, name="w_plane", align_bytes=BURST)
         bias_rows = keep.tile([P, M_TILES, BLOCK], F32, name="bias_rows", align_bytes=64)
         bias = keep.tile([P, M_TILES, BLOCK], F32, name="bias", align_bytes=64)
 
@@ -46,7 +47,7 @@ def tile_picked_grid_lin_bias_sub_l_kernel(tc, xT, w_words, w_scales, b, offs, o
         for first, count in LOADS:
             a, t = divmod(first, PACK)
             rows = xT[a * K_PASS : (a + 1) * K_PASS, :].rearrange("(p t) c -> p (t c)", t=PACK)
-            tables = keep.tile([P, count * T], F32, name="tables%d" % first)
+            tables = keep.tile([P, count * T], F32, name="tables%d" % first, align_bytes=BURST)
             nc.sync.dma_start(tables[:], rows[:, t * T : (t + count) * T])
             windows.extend(tables[:, j * T : (j + 1) * T] for j in range(count))
 
@@ -98,7 +99,7 @@ def tile_picked_grid_lin_bias_sub_l_kernel(tc, xT, w_words, w_scales, b, offs, o
         for c in range(M_TILES):
             nc.vector.transpose(bias[:, c, :], bias_rows[:, c, :])
         for c in range(M_TILES):
-            result = keep.tile([P, V], F32, name="result%d" % c)
+            result = keep.tile([P, V], F32, name="result%d" % c, align_bytes=BURST)
             nc.scalar.activation(result[:, halves[1]], sums[1][c][:], IDENTITY, bias=bias[:, c, 0:1])
             nc.vector.tensor_scalar_add(result[:, halves[0]], sums[0][c][:], bias[:, c, 0:1])
             nc.sync.dma_start(out[c * P : (c + 1) * P, :], result[:])

@@ -21,10 +21,13 @@ PASSES = K // K_PASS
 M_TILES = N // P
 LIST_COLS = V // 16
 HALF = V // 2
+QUADRANT = 32
+SCALE_ROWS = 4
+PAIR = 2
+MX_ALIGN = 64
+DMA_ALIGN = 256
+
 LOADS = ((0, 4), (4, 2), (6, 1), (7, 1))
-BLOCK = 32
-BURST = 256
-PAIRED = 2
 
 
 def tile_picked_grid_lin_bias_sub_l_kernel(tc, xT, w_words, w_scales, b, offs, out):
@@ -33,54 +36,57 @@ def tile_picked_grid_lin_bias_sub_l_kernel(tc, xT, w_words, w_scales, b, offs, o
         keep = ctx.enter_context(tc.tile_pool(name="keep", bufs=1))
         psum = ctx.enter_context(tc.psum_pool(name="psum", bufs=1))
 
-        offsets = keep.tile([P, D * LIST_COLS], U16, name="offsets", align_bytes=BURST)
-        w_codes = keep.tile([P, PASSES, N], U32, name="w_codes", align_bytes=BURST)
-        w_plane = keep.tile([P, PASSES, N], U8, name="w_plane", align_bytes=BURST)
-        bias_rows = keep.tile([P, M_TILES, BLOCK], F32, name="bias_rows", align_bytes=64)
-        bias = keep.tile([P, M_TILES, BLOCK], F32, name="bias", align_bytes=64)
+        offsets = keep.tile([P, D * LIST_COLS], U16, name="offsets", align_bytes=DMA_ALIGN)
+        w_codes = keep.tile([P, PASSES, N], U32, name="w_codes", align_bytes=DMA_ALIGN)
+        w_scale_bytes = keep.tile([P, PASSES, N], U8, name="w_scale_bytes", align_bytes=DMA_ALIGN)
+        bias_rows = keep.tile([P, M_TILES, QUADRANT], F32, name="bias_rows", align_bytes=MX_ALIGN)
+        bias = keep.tile([P, M_TILES, QUADRANT], F32, name="bias", align_bytes=MX_ALIGN)
 
-        nc.vector.memset(w_plane[:].rearrange("p a m -> p (a m)").bitcast(I32), 0)
         nc.vector.memset(bias_rows[:], 0.0)
+        nc.vector.memset(w_scale_bytes[:].rearrange("p a m -> p (a m)").bitcast(I32), 0)
 
         nc.sync.dma_start(offsets[:], offs)
         windows = []
         for first, count in LOADS:
             a, t = divmod(first, PACK)
             rows = xT[a * K_PASS : (a + 1) * K_PASS, :].rearrange("(p t) c -> p (t c)", t=PACK)
-            tables = keep.tile([P, count * T], F32, name="tables%d" % first, align_bytes=BURST)
+            tables = keep.tile([P, count * T], F32, name="tables%d" % first, align_bytes=DMA_ALIGN)
             nc.sync.dma_start(tables[:], rows[:, t * T : (t + count) * T])
+            if first == 0:
+                nc.sync.dma_start(
+                    bias_rows[0:P:QUADRANT, :, :],
+                    b.rearrange("(c q j) o -> q c (j o)", c=M_TILES, j=QUADRANT),
+                )
             windows.extend(tables[:, j * T : (j + 1) * T] for j in range(count))
 
         words = w_words.rearrange("a p m r -> a p (m r)")
-        nc.sync.dma_start(w_codes[:, 0, :].bitcast(I32), words[0].bitcast(I32))
-        for q in range(4):
-            nc.sync.dma_start(
-                w_plane[32 * q : 32 * q + 4, :, :].bitcast(I32),
-                w_scales[:, 4 * q : 4 * q + 4, :].rearrange("a r m -> r a m").bitcast(I32),
-            )
+        nc.sync.dma_start(w_codes[:, 0, 0:P].bitcast(I32), words[0].bitcast(I32)[:, 0:P])
+        scale_rows = w_scales.rearrange("a (q r) m -> r q a m", r=SCALE_ROWS)
+        for r in range(SCALE_ROWS):
+            nc.sync.dma_start(w_scale_bytes[r:P:QUADRANT, :, :].bitcast(I32), scale_rows[r].bitcast(I32))
+        nc.sync.dma_start(w_codes[:, 0, P:N].bitcast(I32), words[0].bitcast(I32)[:, P:N])
         nc.sync.dma_start(w_codes[:, 1, :].bitcast(I32), words[1].bitcast(I32))
-        nc.sync.dma_start(bias_rows[0:P:BLOCK, :, :], b.rearrange("(c q j) o -> q c (j o)", c=M_TILES, j=BLOCK))
 
-        picked = keep.tile([P, PAIRED, V], F32, name="picked")
+        picked = keep.tile([P, PAIR, V], F32, name="picked")
         halves = [slice(h * HALF, (h + 1) * HALF) for h in range(2)]
         sums = [[psum.tile([P, HALF], F32, name="sums%d_%d" % (h, c)) for c in range(M_TILES)] for h in range(2)]
         for a in range(PASSES):
-            grouped = keep.tile([P, V, PACK], BF16, name="grouped%d" % a, align_bytes=64)
+            grouped = keep.tile([P, V, PACK], BF16, name="grouped%d" % a, align_bytes=MX_ALIGN)
             for t in range(PACK):
                 level = PACK * a + t
                 piece = offsets[:, level * LIST_COLS : (level + 1) * LIST_COLS]
-                if a == 0 and t < PAIRED:
+                if level < PAIR:
                     nc.vector.tensor_copy(picked[:, t, :], windows[level].indirect(piece))
-                    if t == PAIRED - 1:
-                        nc.scalar.activation(grouped[:, :, 0:PAIRED], picked[:].rearrange("p t v -> p v t"), IDENTITY)
+                    if level == PAIR - 1:
+                        nc.scalar.activation(grouped[:, :, 0:PAIR], picked[:].rearrange("p t v -> p v t"), IDENTITY)
                 else:
                     nc.vector.tensor_copy(grouped[:, :, t], windows[level].indirect(piece))
-            x_codes = keep.tile([P, V], U32, name="x_codes%d" % a, align_bytes=64)
-            x_plane = keep.tile([P, V], U8, name="x_plane%d" % a, align_bytes=64)
+            x_codes = keep.tile([P, V], U32, name="x_codes%d" % a, align_bytes=MX_ALIGN)
+            x_scale_bytes = keep.tile([P, V], U8, name="x_scale_bytes%d" % a, align_bytes=MX_ALIGN)
             for points in halves:
                 nc.vector.quantize_mx(
                     out=x_codes[:, points].bitcast(FP8X4),
-                    scales=x_plane[:, points],
+                    scales=x_scale_bytes[:, points],
                     in_=grouped[:, points, :].rearrange("p v t -> p (v t)"),
                 )
             for c in range(M_TILES):
@@ -89,9 +95,9 @@ def tile_picked_grid_lin_bias_sub_l_kernel(tc, xT, w_words, w_scales, b, offs, o
                     nc.tensor.matmul_mx(
                         out=sums[h][c][:],
                         lhsT=w_codes[:, a, cols].bitcast(FP8X4),
-                        lhsT_scale=w_plane[:, a, cols],
+                        lhsT_scale=w_scale_bytes[:, a, cols],
                         rhs=x_codes[:, points].bitcast(FP8X4),
-                        rhs_scale=x_plane[:, points],
+                        rhs_scale=x_scale_bytes[:, points],
                         start=(a == 0),
                         stop=(a == PASSES - 1),
                     )
@@ -99,7 +105,7 @@ def tile_picked_grid_lin_bias_sub_l_kernel(tc, xT, w_words, w_scales, b, offs, o
         for c in range(M_TILES):
             nc.vector.transpose(bias[:, c, :], bias_rows[:, c, :])
         for c in range(M_TILES):
-            result = keep.tile([P, V], F32, name="result%d" % c, align_bytes=BURST)
+            result = keep.tile([P, V], F32, name="result%d" % c, align_bytes=DMA_ALIGN)
             nc.scalar.activation(result[:, halves[1]], sums[1][c][:], IDENTITY, bias=bias[:, c, 0:1])
             nc.vector.tensor_scalar_add(result[:, halves[0]], sums[0][c][:], bias[:, c, 0:1])
             nc.sync.dma_start(out[c * P : (c + 1) * P, :], result[:])

@@ -22,6 +22,7 @@ M_TILES = N // P
 LIST_COLS = V // 16
 HALF = V // 2
 QUADRANT = 32
+BIAS_STEP = QUADRANT // M_TILES
 SCALE_ROWS = 4
 PAIR = 2
 MX_ALIGN = 64
@@ -39,11 +40,16 @@ def tile_picked_grid_lin_bias_sub_l_kernel(tc, xT, w_words, w_scales, b, offs, o
         offsets = keep.tile([P, D * LIST_COLS], U16, name="offsets", align_bytes=DMA_ALIGN)
         w_codes = keep.tile([P, PASSES, N], U32, name="w_codes", align_bytes=DMA_ALIGN)
         w_scale_bytes = keep.tile([P, PASSES, N], U8, name="w_scale_bytes", align_bytes=DMA_ALIGN)
-        bias_rows = keep.tile([P, M_TILES, QUADRANT], F32, name="bias_rows", align_bytes=MX_ALIGN)
-        bias = keep.tile([P, M_TILES, QUADRANT], F32, name="bias", align_bytes=MX_ALIGN)
+        bias_rows = keep.tile([P, QUADRANT], F32, name="bias_rows", align_bytes=MX_ALIGN)
+        bias = keep.tile([P, QUADRANT], F32, name="bias", align_bytes=MX_ALIGN)
 
-        nc.vector.memset(bias_rows[:], 0.0)
         nc.vector.memset(w_scale_bytes[:].rearrange("p a m -> p (a m)").bitcast(I32), 0)
+        nc.vector.memset(bias_rows[:], 0.0)
+
+        scale_rows = w_scales.rearrange("a (q r) m -> r q a m", r=SCALE_ROWS)
+
+        def load_scale_rows(r):
+            nc.sync.dma_start(w_scale_bytes[r:P:QUADRANT, :, :].bitcast(I32), scale_rows[r].bitcast(I32))
 
         nc.sync.dma_start(offsets[:], offs)
         windows = []
@@ -53,19 +59,19 @@ def tile_picked_grid_lin_bias_sub_l_kernel(tc, xT, w_words, w_scales, b, offs, o
             tables = keep.tile([P, count * T], F32, name="tables%d" % first, align_bytes=DMA_ALIGN)
             nc.sync.dma_start(tables[:], rows[:, t * T : (t + count) * T])
             if first == 0:
-                nc.sync.dma_start(
-                    bias_rows[0:P:QUADRANT, :, :],
-                    b.rearrange("(c q j) o -> q c (j o)", c=M_TILES, j=QUADRANT),
-                )
+                load_scale_rows(0)
             windows.extend(tables[:, j * T : (j + 1) * T] for j in range(count))
 
         words = w_words.rearrange("a p m r -> a p (m r)")
         nc.sync.dma_start(w_codes[:, 0, 0:P].bitcast(I32), words[0].bitcast(I32)[:, 0:P])
-        scale_rows = w_scales.rearrange("a (q r) m -> r q a m", r=SCALE_ROWS)
-        for r in range(SCALE_ROWS):
-            nc.sync.dma_start(w_scale_bytes[r:P:QUADRANT, :, :].bitcast(I32), scale_rows[r].bitcast(I32))
+        for r in range(1, SCALE_ROWS):
+            load_scale_rows(r)
         nc.sync.dma_start(w_codes[:, 0, P:N].bitcast(I32), words[0].bitcast(I32)[:, P:N])
         nc.sync.dma_start(w_codes[:, 1, :].bitcast(I32), words[1].bitcast(I32))
+        nc.sync.dma_start(
+            bias_rows[0:P:BIAS_STEP, :],
+            b.rearrange("(c q j) o -> q c (j o)", c=M_TILES, j=QUADRANT),
+        )
 
         picked = keep.tile([P, PAIR, V], F32, name="picked")
         halves = [slice(h * HALF, (h + 1) * HALF) for h in range(2)]
@@ -102,10 +108,10 @@ def tile_picked_grid_lin_bias_sub_l_kernel(tc, xT, w_words, w_scales, b, offs, o
                         stop=(a == PASSES - 1),
                     )
 
-        for c in range(M_TILES):
-            nc.vector.transpose(bias[:, c, :], bias_rows[:, c, :])
+        nc.vector.transpose(bias[:], bias_rows[:])
         for c in range(M_TILES):
             result = keep.tile([P, V], F32, name="result%d" % c, align_bytes=DMA_ALIGN)
-            nc.scalar.activation(result[:, halves[1]], sums[1][c][:], IDENTITY, bias=bias[:, c, 0:1])
-            nc.vector.tensor_scalar_add(result[:, halves[0]], sums[0][c][:], bias[:, c, 0:1])
+            column = bias[:, c * BIAS_STEP : c * BIAS_STEP + 1]
+            nc.scalar.activation(result[:, halves[1]], sums[1][c][:], IDENTITY, bias=column)
+            nc.vector.tensor_scalar_add(result[:, halves[0]], sums[0][c][:], column)
             nc.sync.dma_start(out[c * P : (c + 1) * P, :], result[:])

@@ -12,7 +12,6 @@ U32 = mybir.dt.uint32
 U16 = mybir.dt.uint16
 U8 = mybir.dt.uint8
 FP8X4 = mybir.dt.float8_e4m3fn_x4
-IDENTITY = mybir.ActivationFunctionType.Identity
 
 P = 128
 PACK = 4
@@ -24,7 +23,6 @@ HALF = V // 2
 QUADRANT = 32
 BIAS_STEP = QUADRANT // M_TILES
 SCALE_ROWS = 4
-PAIR = 2
 MX_ALIGN = 64
 DMA_ALIGN = 256
 
@@ -43,13 +41,13 @@ def tile_picked_grid_lin_bias_sub_l_kernel(tc, xT, w_words, w_scales, b, offs, o
         bias_rows = keep.tile([P, QUADRANT], F32, name="bias_rows", align_bytes=MX_ALIGN)
         bias = keep.tile([P, QUADRANT], F32, name="bias", align_bytes=MX_ALIGN)
 
-        nc.vector.memset(w_scale_bytes[:].rearrange("p a m -> p (a m)").bitcast(I32), 0)
         nc.vector.memset(bias_rows[:], 0.0)
+        nc.vector.memset(w_scale_bytes[:].rearrange("p a m -> p (a m)").bitcast(I32), 0)
 
         scale_rows = w_scales.rearrange("a (q r) m -> r q a m", r=SCALE_ROWS)
 
         def load_scale_rows(r):
-            nc.sync.dma_start(w_scale_bytes[r:P:QUADRANT, :, :].bitcast(I32), scale_rows[r].bitcast(I32))
+            nc.scalar.dma_start(w_scale_bytes[r:P:QUADRANT, :, :].bitcast(I32), scale_rows[r].bitcast(I32))
 
         nc.sync.dma_start(offsets[:], offs)
         windows = []
@@ -57,23 +55,21 @@ def tile_picked_grid_lin_bias_sub_l_kernel(tc, xT, w_words, w_scales, b, offs, o
             a, t = divmod(first, PACK)
             rows = xT[a * K_PASS : (a + 1) * K_PASS, :].rearrange("(p t) c -> p (t c)", t=PACK)
             tables = keep.tile([P, count * T], F32, name="tables%d" % first, align_bytes=DMA_ALIGN)
-            nc.sync.dma_start(tables[:], rows[:, t * T : (t + count) * T])
+            nc.scalar.dma_start(tables[:], rows[:, t * T : (t + count) * T])
             if first == 0:
-                load_scale_rows(0)
+                nc.scalar.dma_start(
+                    bias_rows[0:P:BIAS_STEP, :],
+                    b.rearrange("(c q j) o -> q c (j o)", c=M_TILES, j=QUADRANT),
+                )
             windows.extend(tables[:, j * T : (j + 1) * T] for j in range(count))
 
         words = w_words.rearrange("a p m r -> a p (m r)")
-        nc.sync.dma_start(w_codes[:, 0, 0:P].bitcast(I32), words[0].bitcast(I32)[:, 0:P])
-        for r in range(1, SCALE_ROWS):
+        nc.scalar.dma_start(w_codes[:, 0, 0:P].bitcast(I32), words[0].bitcast(I32)[:, 0:P])
+        for r in range(SCALE_ROWS):
             load_scale_rows(r)
-        nc.sync.dma_start(w_codes[:, 0, P:N].bitcast(I32), words[0].bitcast(I32)[:, P:N])
-        nc.sync.dma_start(w_codes[:, 1, :].bitcast(I32), words[1].bitcast(I32))
-        nc.sync.dma_start(
-            bias_rows[0:P:BIAS_STEP, :],
-            b.rearrange("(c q j) o -> q c (j o)", c=M_TILES, j=QUADRANT),
-        )
+        nc.scalar.dma_start(w_codes[:, 0, P:N].bitcast(I32), words[0].bitcast(I32)[:, P:N])
+        nc.scalar.dma_start(w_codes[:, 1, :].bitcast(I32), words[1].bitcast(I32))
 
-        picked = keep.tile([P, PAIR, V], F32, name="picked")
         halves = [slice(h * HALF, (h + 1) * HALF) for h in range(2)]
         sums = [[psum.tile([P, HALF], F32, name="sums%d_%d" % (h, c)) for c in range(M_TILES)] for h in range(2)]
         for a in range(PASSES):
@@ -81,12 +77,7 @@ def tile_picked_grid_lin_bias_sub_l_kernel(tc, xT, w_words, w_scales, b, offs, o
             for t in range(PACK):
                 level = PACK * a + t
                 piece = offsets[:, level * LIST_COLS : (level + 1) * LIST_COLS]
-                if level < PAIR:
-                    nc.vector.tensor_copy(picked[:, t, :], windows[level].indirect(piece))
-                    if level == PAIR - 1:
-                        nc.scalar.activation(grouped[:, :, 0:PAIR], picked[:].rearrange("p t v -> p v t"), IDENTITY)
-                else:
-                    nc.vector.tensor_copy(grouped[:, :, t], windows[level].indirect(piece))
+                nc.vector.tensor_copy(grouped[:, :, t], windows[level].indirect(piece))
             x_codes = keep.tile([P, V], U32, name="x_codes%d" % a, align_bytes=MX_ALIGN)
             x_scale_bytes = keep.tile([P, V], U8, name="x_scale_bytes%d" % a, align_bytes=MX_ALIGN)
             for points in halves:
@@ -112,6 +103,6 @@ def tile_picked_grid_lin_bias_sub_l_kernel(tc, xT, w_words, w_scales, b, offs, o
         for c in range(M_TILES):
             result = keep.tile([P, V], F32, name="result%d" % c, align_bytes=DMA_ALIGN)
             column = bias[:, c * BIAS_STEP : c * BIAS_STEP + 1]
-            nc.scalar.activation(result[:, halves[1]], sums[1][c][:], IDENTITY, bias=column)
-            nc.vector.tensor_scalar_add(result[:, halves[0]], sums[0][c][:], column)
+            for h, points in enumerate(halves):
+                nc.vector.tensor_scalar_add(result[:, points], sums[h][c][:], column)
             nc.sync.dma_start(out[c * P : (c + 1) * P, :], result[:])

@@ -47,7 +47,7 @@ def tile_picked_grid_lin_bias_sub_l_kernel(tc, xT, w_words, w_scales, b, offs, o
         scale_rows = w_scales.rearrange("a (q r) m -> r q a m", r=SCALE_ROWS)
 
         def load_scale_rows(r):
-            nc.scalar.dma_start(w_scale_bytes[r:P:QUADRANT, :, :].bitcast(I32), scale_rows[r].bitcast(I32))
+            nc.sync.dma_start(w_scale_bytes[r:P:QUADRANT, :, :].bitcast(I32), scale_rows[r].bitcast(I32))
 
         nc.sync.dma_start(offsets[:], offs)
         windows = []
@@ -55,20 +55,20 @@ def tile_picked_grid_lin_bias_sub_l_kernel(tc, xT, w_words, w_scales, b, offs, o
             a, t = divmod(first, PACK)
             rows = xT[a * K_PASS : (a + 1) * K_PASS, :].rearrange("(p t) c -> p (t c)", t=PACK)
             tables = keep.tile([P, count * T], F32, name="tables%d" % first, align_bytes=DMA_ALIGN)
-            nc.scalar.dma_start(tables[:], rows[:, t * T : (t + count) * T])
+            nc.sync.dma_start(tables[:], rows[:, t * T : (t + count) * T])
             if first == 0:
-                nc.scalar.dma_start(
+                nc.sync.dma_start(
                     bias_rows[0:P:BIAS_STEP, :],
                     b.rearrange("(c q j) o -> q c (j o)", c=M_TILES, j=QUADRANT),
                 )
             windows.extend(tables[:, j * T : (j + 1) * T] for j in range(count))
 
         words = w_words.rearrange("a p m r -> a p (m r)")
-        nc.scalar.dma_start(w_codes[:, 0, 0:P].bitcast(I32), words[0].bitcast(I32)[:, 0:P])
+        nc.sync.dma_start(w_codes[:, 0, 0:P].bitcast(I32), words[0].bitcast(I32)[:, 0:P])
         for r in range(SCALE_ROWS):
             load_scale_rows(r)
-        nc.scalar.dma_start(w_codes[:, 0, P:N].bitcast(I32), words[0].bitcast(I32)[:, P:N])
-        nc.scalar.dma_start(w_codes[:, 1, :].bitcast(I32), words[1].bitcast(I32))
+        nc.sync.dma_start(w_codes[:, 0, P:N].bitcast(I32), words[0].bitcast(I32)[:, P:N])
+        nc.sync.dma_start(w_codes[:, 1, :].bitcast(I32), words[1].bitcast(I32))
 
         halves = [slice(h * HALF, (h + 1) * HALF) for h in range(2)]
         sums = [[psum.tile([P, HALF], F32, name="sums%d_%d" % (h, c)) for c in range(M_TILES)] for h in range(2)]

@@ -56,19 +56,17 @@ def tile_picked_grid_lin_bias_sub_l_kernel(tc, xT, w_words, w_scales, b, offs, o
             rows = xT[a * K_PASS : (a + 1) * K_PASS, :].rearrange("(p t) c -> p (t c)", t=PACK)
             tables = keep.tile([P, count * T], F32, name="tables%d" % first, align_bytes=DMA_ALIGN)
             nc.sync.dma_start(tables[:], rows[:, t * T : (t + count) * T])
-            if first == 0:
-                nc.sync.dma_start(
-                    bias_rows[0:P:BIAS_STEP, :],
-                    b.rearrange("(c q j) o -> q c (j o)", c=M_TILES, j=QUADRANT),
-                )
             windows.extend(tables[:, j * T : (j + 1) * T] for j in range(count))
 
         words = w_words.rearrange("a p m r -> a p (m r)")
-        nc.sync.dma_start(w_codes[:, 0, 0:P].bitcast(I32), words[0].bitcast(I32)[:, 0:P])
+        nc.sync.dma_start(w_codes[:, 0, :].bitcast(I32), words[0].bitcast(I32))
         for r in range(SCALE_ROWS):
             load_scale_rows(r)
-        nc.sync.dma_start(w_codes[:, 0, P:N].bitcast(I32), words[0].bitcast(I32)[:, P:N])
         nc.sync.dma_start(w_codes[:, 1, :].bitcast(I32), words[1].bitcast(I32))
+        nc.sync.dma_start(
+            bias_rows[0:P:BIAS_STEP, :],
+            b.rearrange("(c q j) o -> q c (j o)", c=M_TILES, j=QUADRANT),
+        )
 
         halves = [slice(h * HALF, (h + 1) * HALF) for h in range(2)]
         sums = [[psum.tile([P, HALF], F32, name="sums%d_%d" % (h, c)) for c in range(M_TILES)] for h in range(2)]

@@ -26,8 +26,6 @@ SCALE_ROWS = 4
 MX_ALIGN = 64
 DMA_ALIGN = 256
 
-LOADS = ((0, 4), (4, 2), (6, 1), (7, 1))
-
 
 def tile_picked_grid_lin_bias_sub_l_kernel(tc, xT, w_words, w_scales, b, offs, out):
     nc = tc.nc
@@ -40,67 +38,86 @@ def tile_picked_grid_lin_bias_sub_l_kernel(tc, xT, w_words, w_scales, b, offs, o
         w_scale_bytes = keep.tile([P, PASSES, N], U8, name="w_scale_bytes", align_bytes=DMA_ALIGN)
         bias_rows = keep.tile([P, QUADRANT], F32, name="bias_rows", align_bytes=MX_ALIGN)
         bias = keep.tile([P, QUADRANT], F32, name="bias", align_bytes=MX_ALIGN)
-
         nc.vector.memset(bias_rows[:], 0.0)
         nc.vector.memset(w_scale_bytes[:].rearrange("p a m -> p (a m)").bitcast(I32), 0)
 
+        windows = {}
+        words = w_words.rearrange("a p m r -> p a (m r)").bitcast(I32)
         scale_rows = w_scales.rearrange("a (q r) m -> r q a m", r=SCALE_ROWS)
 
-        def load_scale_rows(r):
-            nc.sync.dma_start(w_scale_bytes[r:P:QUADRANT, :, :].bitcast(I32), scale_rows[r].bitcast(I32))
-
-        nc.sync.dma_start(offsets[:], offs)
-        windows = []
-        for first, count in LOADS:
+        def load_tables(first, count):
             a, t = divmod(first, PACK)
             rows = xT[a * K_PASS : (a + 1) * K_PASS, :].rearrange("(p t) c -> p (t c)", t=PACK)
             tables = keep.tile([P, count * T], F32, name="tables%d" % first, align_bytes=DMA_ALIGN)
             nc.sync.dma_start(tables[:], rows[:, t * T : (t + count) * T])
-            windows.extend(tables[:, j * T : (j + 1) * T] for j in range(count))
+            for j in range(count):
+                windows[first + j] = tables[:, j * T : (j + 1) * T]
 
-        words = w_words.rearrange("a p m r -> a p (m r)")
-        nc.sync.dma_start(w_codes[:, 0, :].bitcast(I32), words[0].bitcast(I32))
-        for r in range(SCALE_ROWS):
-            load_scale_rows(r)
-        nc.sync.dma_start(w_codes[:, 1, :].bitcast(I32), words[1].bitcast(I32))
-        nc.sync.dma_start(
-            bias_rows[0:P:BIAS_STEP, :],
-            b.rearrange("(c q j) o -> q c (j o)", c=M_TILES, j=QUADRANT),
-        )
+        def load_codes(passes, cols):
+            nc.sync.dma_start(w_codes[:, passes, cols].bitcast(I32), words[:, passes, cols])
+
+        def load_scale_rows(r):
+            nc.sync.dma_start(w_scale_bytes[r:P:QUADRANT, :, :].bitcast(I32), scale_rows[r].bitcast(I32))
+
+        def load_bias():
+            nc.sync.dma_start(
+                bias_rows[0:P:BIAS_STEP, :],
+                b.rearrange("(c q j) o -> q c (j o)", c=M_TILES, j=QUADRANT),
+            )
+
+        nc.sync.dma_start(offsets[:], offs)
+        load_tables(0, 4)
+        load_scale_rows(0)
+        load_scale_rows(1)
+        load_tables(4, 2)
+        load_scale_rows(2)
+        load_tables(6, 1)
+        load_scale_rows(3)
+        load_tables(7, 1)
+        for c in range(M_TILES):
+            load_codes(slice(0, 1), slice(c * P, (c + 1) * P))
+        load_codes(slice(1, 2), slice(0, N))
+        load_bias()
 
         halves = [slice(h * HALF, (h + 1) * HALF) for h in range(2)]
-        sums = [[psum.tile([P, HALF], F32, name="sums%d_%d" % (h, c)) for c in range(M_TILES)] for h in range(2)]
+        tiles = [slice(c * P, (c + 1) * P) for c in range(M_TILES)]
+        x_codes, x_scale_bytes = [], []
         for a in range(PASSES):
             grouped = keep.tile([P, V, PACK], BF16, name="grouped%d" % a, align_bytes=MX_ALIGN)
             for t in range(PACK):
                 level = PACK * a + t
                 piece = offsets[:, level * LIST_COLS : (level + 1) * LIST_COLS]
                 nc.vector.tensor_copy(grouped[:, :, t], windows[level].indirect(piece))
-            x_codes = keep.tile([P, V], U32, name="x_codes%d" % a, align_bytes=MX_ALIGN)
-            x_scale_bytes = keep.tile([P, V], U8, name="x_scale_bytes%d" % a, align_bytes=MX_ALIGN)
+            x_codes.append(keep.tile([P, V], U32, name="x_codes%d" % a, align_bytes=MX_ALIGN))
+            x_scale_bytes.append(keep.tile([P, V], U8, name="x_scale_bytes%d" % a, align_bytes=MX_ALIGN))
             for points in halves:
                 nc.vector.quantize_mx(
-                    out=x_codes[:, points].bitcast(FP8X4),
-                    scales=x_scale_bytes[:, points],
+                    out=x_codes[a][:, points].bitcast(FP8X4),
+                    scales=x_scale_bytes[a][:, points],
                     in_=grouped[:, points, :].rearrange("p v t -> p (v t)"),
                 )
+
+        def multiply(bank, a, c, points, start, stop):
+            nc.tensor.matmul_mx(
+                out=bank,
+                lhsT=w_codes[:, a, tiles[c]].bitcast(FP8X4),
+                lhsT_scale=w_scale_bytes[:, a, tiles[c]],
+                rhs=x_codes[a][:, points].bitcast(FP8X4),
+                rhs_scale=x_scale_bytes[a][:, points],
+                start=start,
+                stop=stop,
+            )
+
+        sums = [[psum.tile([P, HALF], F32, name="sums%d_%d" % (c, h)) for h in range(2)] for c in range(M_TILES)]
+        for a in range(PASSES):
             for c in range(M_TILES):
                 for h, points in enumerate(halves):
-                    cols = slice(c * P, (c + 1) * P)
-                    nc.tensor.matmul_mx(
-                        out=sums[h][c][:],
-                        lhsT=w_codes[:, a, cols].bitcast(FP8X4),
-                        lhsT_scale=w_scale_bytes[:, a, cols],
-                        rhs=x_codes[:, points].bitcast(FP8X4),
-                        rhs_scale=x_scale_bytes[:, points],
-                        start=(a == 0),
-                        stop=(a == PASSES - 1),
-                    )
+                    multiply(sums[c][h][:], a, c, points, a == 0, a == PASSES - 1)
 
         nc.vector.transpose(bias[:], bias_rows[:])
         for c in range(M_TILES):
             result = keep.tile([P, V], F32, name="result%d" % c, align_bytes=DMA_ALIGN)
             column = bias[:, c * BIAS_STEP : c * BIAS_STEP + 1]
             for h, points in enumerate(halves):
-                nc.vector.tensor_scalar_add(result[:, points], sums[h][c][:], column)
-            nc.sync.dma_start(out[c * P : (c + 1) * P, :], result[:])
+                nc.vector.tensor_scalar_add(result[:, points], sums[c][h][:], column)
+            nc.sync.dma_start(out[tiles[c], :], result[:])

@@ -13,6 +13,8 @@ U16 = mybir.dt.uint16
 U8 = mybir.dt.uint8
 FP8X4 = mybir.dt.float8_e4m3fn_x4
 
+COPY = mybir.ActivationFunctionType.Copy
+
 P = 128
 PACK = 4
 K_PASS = P * PACK
@@ -20,6 +22,8 @@ PASSES = K // K_PASS
 M_TILES = N // P
 LIST_COLS = V // 16
 HALF = V // 2
+QUARTER = V // 4
+QUARTER_COLS = LIST_COLS // 4
 QUADRANT = 32
 BIAS_STEP = QUADRANT // M_TILES
 SCALE_ROWS = 4
@@ -87,7 +91,21 @@ def tile_picked_grid_lin_bias_sub_l_kernel(tc, xT, w_words, w_scales, b, offs, o
             for t in range(PACK):
                 level = PACK * a + t
                 piece = offsets[:, level * LIST_COLS : (level + 1) * LIST_COLS]
-                nc.vector.tensor_copy(grouped[:, :, t], windows[level].indirect(piece))
+                if level < D - 1:
+                    nc.vector.tensor_copy(grouped[:, :, t], windows[level].indirect(piece))
+                    continue
+                plain = keep.tile([P, V], BF16, name="plain", align_bytes=MX_ALIGN)
+                for h, points in enumerate(halves):
+                    for e in range(2):
+                        q = 2 * h + e
+                        quarter = plain[:, q * QUARTER : (q + 1) * QUARTER]
+                        looked_up = windows[level].indirect(piece[:, q * QUARTER_COLS : (q + 1) * QUARTER_COLS])
+                        if e == 0:
+                            nc.vector.tensor_copy(quarter, looked_up)
+                        else:
+                            nc.scalar.activation(quarter, looked_up, COPY)
+                for points in halves:
+                    nc.vector.tensor_copy(grouped[:, points, t], plain[:, points])
             x_codes.append(keep.tile([P, V], U32, name="x_codes%d" % a, align_bytes=MX_ALIGN))
             x_scale_bytes.append(keep.tile([P, V], U8, name="x_scale_bytes%d" % a, align_bytes=MX_ALIGN))
             for points in halves:

@@ -38,9 +38,9 @@ def tile_picked_grid_lin_bias_sub_l_kernel(tc, xT, w_words, w_scales, b, offs, o
         psum = ctx.enter_context(tc.psum_pool(name="psum", bufs=1))
 
         offsets = keep.tile([P, D * LIST_COLS], U16, name="offsets", align_bytes=DMA_ALIGN)
-        w_codes = keep.tile([P, PASSES, N], U32, name="w_codes", align_bytes=DMA_ALIGN)
+        w_codes = {}
         w_scale_bytes = keep.tile([P, PASSES, N], U8, name="w_scale_bytes", align_bytes=DMA_ALIGN)
-        bias_rows = keep.tile([P, QUADRANT], F32, name="bias_rows", align_bytes=MX_ALIGN)
+        bias_rows = keep.tile([P, QUADRANT], F32, name="bias_rows", tag="reused", align_bytes=DMA_ALIGN)
         bias = keep.tile([P, QUADRANT], F32, name="bias", align_bytes=MX_ALIGN)
         nc.vector.memset(bias_rows[:], 0.0)
         nc.vector.memset(w_scale_bytes[:].rearrange("p a m -> p (a m)").bitcast(I32), 0)
@@ -52,13 +52,15 @@ def tile_picked_grid_lin_bias_sub_l_kernel(tc, xT, w_words, w_scales, b, offs, o
         def load_tables(first, count):
             a, t = divmod(first, PACK)
             rows = xT[a * K_PASS : (a + 1) * K_PASS, :].rearrange("(p t) c -> p (t c)", t=PACK)
-            tables = keep.tile([P, count * T], F32, name="tables%d" % first, align_bytes=DMA_ALIGN)
+            tables = keep.tile([P, count * T], F32, name="tables%d" % first, tag="tables%d" % first, align_bytes=DMA_ALIGN)
             nc.sync.dma_start(tables[:], rows[:, t * T : (t + count) * T])
             for j in range(count):
                 windows[first + j] = tables[:, j * T : (j + 1) * T]
 
-        def load_codes(passes, cols):
-            nc.sync.dma_start(w_codes[:, passes, cols].bitcast(I32), words[:, passes, cols])
+        def load_codes(a, tag):
+            codes = keep.tile([P, N], U32, name="w_codes%d" % a, tag=tag, align_bytes=DMA_ALIGN)
+            nc.sync.dma_start(codes[:].bitcast(I32), words[:, a, :])
+            w_codes[a] = codes
 
         def load_scale_rows(r):
             nc.sync.dma_start(w_scale_bytes[r:P:QUADRANT, :, :].bitcast(I32), scale_rows[r].bitcast(I32))
@@ -69,19 +71,18 @@ def tile_picked_grid_lin_bias_sub_l_kernel(tc, xT, w_words, w_scales, b, offs, o
                 b.rearrange("(c q j) o -> q c (j o)", c=M_TILES, j=QUADRANT),
             )
 
-        nc.sync.dma_start(offsets[:], offs)
         load_tables(0, 4)
-        load_scale_rows(0)
-        load_scale_rows(1)
-        load_tables(4, 2)
-        load_scale_rows(2)
-        load_tables(6, 1)
-        load_scale_rows(3)
-        load_tables(7, 1)
-        for c in range(M_TILES):
-            load_codes(slice(0, 1), slice(c * P, (c + 1) * P))
-        load_codes(slice(1, 2), slice(0, N))
+        nc.sync.dma_start(offsets[:], offs)
+        for r in range(SCALE_ROWS - 1):
+            load_scale_rows(r)
         load_bias()
+        nc.vector.transpose(bias[:], bias_rows[:])
+        load_tables(4, 2)
+        load_scale_rows(SCALE_ROWS - 1)
+        load_tables(6, 1)
+        load_tables(7, 1)
+        load_codes(0, "reused")
+        load_codes(1, "tables4")
 
         halves = [slice(h * HALF, (h + 1) * HALF) for h in range(2)]
         tiles = [slice(c * P, (c + 1) * P) for c in range(M_TILES)]
@@ -118,7 +119,7 @@ def tile_picked_grid_lin_bias_sub_l_kernel(tc, xT, w_words, w_scales, b, offs, o
         def multiply(bank, a, c, points, start, stop):
             nc.tensor.matmul_mx(
                 out=bank,
-                lhsT=w_codes[:, a, tiles[c]].bitcast(FP8X4),
+                lhsT=w_codes[a][:, tiles[c]].bitcast(FP8X4),
                 lhsT_scale=w_scale_bytes[:, a, tiles[c]],
                 rhs=x_codes[a][:, points].bitcast(FP8X4),
                 rhs_scale=x_scale_bytes[a][:, points],
@@ -132,10 +133,12 @@ def tile_picked_grid_lin_bias_sub_l_kernel(tc, xT, w_words, w_scales, b, offs, o
                 for h, points in enumerate(halves):
                     multiply(sums[c][h][:], a, c, points, a == 0, a == PASSES - 1)
 
-        nc.vector.transpose(bias[:], bias_rows[:])
         for c in range(M_TILES):
             result = keep.tile([P, V], F32, name="result%d" % c, align_bytes=DMA_ALIGN)
             column = bias[:, c * BIAS_STEP : c * BIAS_STEP + 1]
             for h, points in enumerate(halves):
                 nc.vector.tensor_scalar_add(result[:, points], sums[c][h][:], column)
-            nc.sync.dma_start(out[tiles[c], :], result[:])
+                if c == 0:
+                    nc.sync.dma_start(out[tiles[c], points], result[:, points])
+            if c > 0:
+                nc.sync.dma_start(out[tiles[c], :], result[:])

@@ -38,13 +38,15 @@ def tile_picked_grid_lin_bias_sub_l_kernel(tc, xT, w_words, w_scales, b, offs, o
         psum = ctx.enter_context(tc.psum_pool(name="psum", bufs=1))
 
         offsets = keep.tile([P, D * LIST_COLS], U16, name="offsets", align_bytes=DMA_ALIGN)
-        w_codes = {}
+        w_codes = keep.tile([P, PASSES, N], U32, name="w_codes", align_bytes=DMA_ALIGN)
         w_scale_bytes = keep.tile([P, PASSES, N], U8, name="w_scale_bytes", align_bytes=DMA_ALIGN)
-        bias_rows = keep.tile([P, QUADRANT], F32, name="bias_rows", tag="reused", align_bytes=DMA_ALIGN)
+        bias_rows = keep.tile([P, QUADRANT], F32, name="bias_rows", align_bytes=DMA_ALIGN)
         bias = keep.tile([P, QUADRANT], F32, name="bias", align_bytes=MX_ALIGN)
         nc.vector.memset(bias_rows[:], 0.0)
         nc.vector.memset(w_scale_bytes[:].rearrange("p a m -> p (a m)").bitcast(I32), 0)
 
+        halves = [slice(h * HALF, (h + 1) * HALF) for h in range(2)]
+        tiles = [slice(c * P, (c + 1) * P) for c in range(M_TILES)]
         windows = {}
         words = w_words.rearrange("a p m r -> p a (m r)").bitcast(I32)
         scale_rows = w_scales.rearrange("a (q r) m -> r q a m", r=SCALE_ROWS)
@@ -52,61 +54,51 @@ def tile_picked_grid_lin_bias_sub_l_kernel(tc, xT, w_words, w_scales, b, offs, o
         def load_tables(first, count):
             a, t = divmod(first, PACK)
             rows = xT[a * K_PASS : (a + 1) * K_PASS, :].rearrange("(p t) c -> p (t c)", t=PACK)
-            tables = keep.tile([P, count * T], F32, name="tables%d" % first, tag="tables%d" % first, align_bytes=DMA_ALIGN)
+            tables = keep.tile([P, count * T], F32, name="tables%d" % first, align_bytes=DMA_ALIGN)
             nc.sync.dma_start(tables[:], rows[:, t * T : (t + count) * T])
             for j in range(count):
                 windows[first + j] = tables[:, j * T : (j + 1) * T]
 
-        def load_codes(a, tag):
-            codes = keep.tile([P, N], U32, name="w_codes%d" % a, tag=tag, align_bytes=DMA_ALIGN)
-            nc.sync.dma_start(codes[:].bitcast(I32), words[:, a, :])
-            w_codes[a] = codes
-
-        def load_scale_rows(r):
-            nc.sync.dma_start(w_scale_bytes[r:P:QUADRANT, :, :].bitcast(I32), scale_rows[r].bitcast(I32))
-
-        def load_bias():
-            nc.sync.dma_start(
-                bias_rows[0:P:BIAS_STEP, :],
-                b.rearrange("(c q j) o -> q c (j o)", c=M_TILES, j=QUADRANT),
-            )
-
         load_tables(0, 4)
         nc.sync.dma_start(offsets[:], offs)
-        for r in range(SCALE_ROWS - 1):
-            load_scale_rows(r)
-        load_bias()
+        nc.sync.dma_start(
+            bias_rows[0:P:BIAS_STEP, :],
+            b.rearrange("(c q j) o -> q c (j o)", c=M_TILES, j=QUADRANT),
+        )
         nc.vector.transpose(bias[:], bias_rows[:])
-        load_tables(4, 2)
-        load_scale_rows(SCALE_ROWS - 1)
-        load_tables(6, 1)
+        load_tables(4, 3)
         load_tables(7, 1)
-        load_codes(0, "reused")
-        load_codes(1, "tables4")
+        for r in range(SCALE_ROWS):
+            nc.sync.dma_start(w_scale_bytes[r:P:QUADRANT, :, :].bitcast(I32), scale_rows[r].bitcast(I32))
+        for cols in tiles:
+            nc.sync.dma_start(w_codes[:, 0, cols].bitcast(I32), words[:, 0, cols])
+        nc.sync.dma_start(w_codes[:, 1, :].bitcast(I32), words[:, 1, :])
 
-        halves = [slice(h * HALF, (h + 1) * HALF) for h in range(2)]
-        tiles = [slice(c * P, (c + 1) * P) for c in range(M_TILES)]
+        def piece(level):
+            return offsets[:, level * LIST_COLS : (level + 1) * LIST_COLS]
+
         x_codes, x_scale_bytes = [], []
         for a in range(PASSES):
             grouped = keep.tile([P, V, PACK], BF16, name="grouped%d" % a, align_bytes=MX_ALIGN)
-            for t in range(PACK):
-                level = PACK * a + t
-                piece = offsets[:, level * LIST_COLS : (level + 1) * LIST_COLS]
-                if level < D - 1:
-                    nc.vector.tensor_copy(grouped[:, :, t], windows[level].indirect(piece))
-                    continue
+            pair = keep.tile([P, 2, V], F32, name="pair%d" % a, align_bytes=MX_ALIGN)
+            for t in range(2):
+                nc.scalar.activation(pair[:, t, :], windows[PACK * a + t].indirect(piece(PACK * a + t)), COPY)
+            nc.vector.tensor_copy(grouped[:, :, 2], windows[PACK * a + 2].indirect(piece(PACK * a + 2)))
+            nc.vector.tensor_copy(grouped[:, :, 0:2], pair[:].rearrange("p t v -> p v t"))
+            level = PACK * a + 3
+            if level < D - 1:
+                nc.vector.tensor_copy(grouped[:, :, 3], windows[level].indirect(piece(level)))
+            else:
                 plain = keep.tile([P, V], BF16, name="plain", align_bytes=MX_ALIGN)
-                for h, points in enumerate(halves):
-                    for e in range(2):
-                        q = 2 * h + e
-                        quarter = plain[:, q * QUARTER : (q + 1) * QUARTER]
-                        looked_up = windows[level].indirect(piece[:, q * QUARTER_COLS : (q + 1) * QUARTER_COLS])
-                        if e == 0:
-                            nc.vector.tensor_copy(quarter, looked_up)
-                        else:
-                            nc.scalar.activation(quarter, looked_up, COPY)
+                for q in range(4):
+                    quarter = plain[:, q * QUARTER : (q + 1) * QUARTER]
+                    looked_up = windows[level].indirect(piece(level)[:, q * QUARTER_COLS : (q + 1) * QUARTER_COLS])
+                    if q % 2 == 0:
+                        nc.vector.tensor_copy(quarter, looked_up)
+                    else:
+                        nc.scalar.activation(quarter, looked_up, COPY)
                 for points in halves:
-                    nc.vector.tensor_copy(grouped[:, points, t], plain[:, points])
+                    nc.vector.tensor_copy(grouped[:, points, 3], plain[:, points])
             x_codes.append(keep.tile([P, V], U32, name="x_codes%d" % a, align_bytes=MX_ALIGN))
             x_scale_bytes.append(keep.tile([P, V], U8, name="x_scale_bytes%d" % a, align_bytes=MX_ALIGN))
             for points in halves:
@@ -116,22 +108,19 @@ def tile_picked_grid_lin_bias_sub_l_kernel(tc, xT, w_words, w_scales, b, offs, o
                     in_=grouped[:, points, :].rearrange("p v t -> p (v t)"),
                 )
 
-        def multiply(bank, a, c, points, start, stop):
-            nc.tensor.matmul_mx(
-                out=bank,
-                lhsT=w_codes[a][:, tiles[c]].bitcast(FP8X4),
-                lhsT_scale=w_scale_bytes[:, a, tiles[c]],
-                rhs=x_codes[a][:, points].bitcast(FP8X4),
-                rhs_scale=x_scale_bytes[a][:, points],
-                start=start,
-                stop=stop,
-            )
-
         sums = [[psum.tile([P, HALF], F32, name="sums%d_%d" % (c, h)) for h in range(2)] for c in range(M_TILES)]
         for a in range(PASSES):
             for c in range(M_TILES):
                 for h, points in enumerate(halves):
-                    multiply(sums[c][h][:], a, c, points, a == 0, a == PASSES - 1)
+                    nc.tensor.matmul_mx(
+                        out=sums[c][h][:],
+                        lhsT=w_codes[:, a, tiles[c]].bitcast(FP8X4),
+                        lhsT_scale=w_scale_bytes[:, a, tiles[c]],
+                        rhs=x_codes[a][:, points].bitcast(FP8X4),
+                        rhs_scale=x_scale_bytes[a][:, points],
+                        start=a == 0,
+                        stop=a == PASSES - 1,
+                    )
 
         for c in range(M_TILES):
             result = keep.tile([P, V], F32, name="result%d" % c, align_bytes=DMA_ALIGN)

@@ -38,9 +38,9 @@ def tile_picked_grid_lin_bias_sub_l_kernel(tc, xT, w_words, w_scales, b, offs, o
         psum = ctx.enter_context(tc.psum_pool(name="psum", bufs=1))
 
         offsets = keep.tile([P, D * LIST_COLS], U16, name="offsets", align_bytes=DMA_ALIGN)
-        w_codes = keep.tile([P, PASSES, N], U32, name="w_codes", align_bytes=DMA_ALIGN)
+        w_codes = {}
         w_scale_bytes = keep.tile([P, PASSES, N], U8, name="w_scale_bytes", align_bytes=DMA_ALIGN)
-        bias_rows = keep.tile([P, QUADRANT], F32, name="bias_rows", align_bytes=DMA_ALIGN)
+        bias_rows = keep.tile([P, QUADRANT], F32, name="bias_rows", tag="reused", align_bytes=DMA_ALIGN)
         bias = keep.tile([P, QUADRANT], F32, name="bias", align_bytes=MX_ALIGN)
         nc.vector.memset(bias_rows[:], 0.0)
         nc.vector.memset(w_scale_bytes[:].rearrange("p a m -> p (a m)").bitcast(I32), 0)
@@ -59,20 +59,30 @@ def tile_picked_grid_lin_bias_sub_l_kernel(tc, xT, w_words, w_scales, b, offs, o
             for j in range(count):
                 windows[first + j] = tables[:, j * T : (j + 1) * T]
 
+        def load_scale_rows(r):
+            nc.sync.dma_start(w_scale_bytes[r:P:QUADRANT, :, :].bitcast(I32), scale_rows[r].bitcast(I32))
+
+        def load_codes(a, first, count, tag):
+            codes = keep.tile([P, count * P], U32, name=tag, tag=tag, align_bytes=DMA_ALIGN)
+            nc.sync.dma_start(codes[:].bitcast(I32), words[:, a, first * P : (first + count) * P])
+            for j in range(count):
+                w_codes[a, first + j] = codes[:, j * P : (j + 1) * P]
+
         load_tables(0, 4)
         nc.sync.dma_start(offsets[:], offs)
+        for r in range(SCALE_ROWS - 1):
+            load_scale_rows(r)
         nc.sync.dma_start(
             bias_rows[0:P:BIAS_STEP, :],
             b.rearrange("(c q j) o -> q c (j o)", c=M_TILES, j=QUADRANT),
         )
         nc.vector.transpose(bias[:], bias_rows[:])
         load_tables(4, 3)
+        load_scale_rows(SCALE_ROWS - 1)
         load_tables(7, 1)
-        for r in range(SCALE_ROWS):
-            nc.sync.dma_start(w_scale_bytes[r:P:QUADRANT, :, :].bitcast(I32), scale_rows[r].bitcast(I32))
-        for cols in tiles:
-            nc.sync.dma_start(w_codes[:, 0, cols].bitcast(I32), words[:, 0, cols])
-        nc.sync.dma_start(w_codes[:, 1, :].bitcast(I32), words[:, 1, :])
+        load_codes(0, 0, 1, "reused")
+        load_codes(0, 1, 1, "w_codes01")
+        load_codes(1, 0, M_TILES, "w_codes1")
 
         def piece(level):
             return offsets[:, level * LIST_COLS : (level + 1) * LIST_COLS]
@@ -114,7 +124,7 @@ def tile_picked_grid_lin_bias_sub_l_kernel(tc, xT, w_words, w_scales, b, offs, o
                 for h, points in enumerate(halves):
                     nc.tensor.matmul_mx(
                         out=sums[c][h][:],
-                        lhsT=w_codes[:, a, tiles[c]].bitcast(FP8X4),
+                        lhsT=w_codes[a, c].bitcast(FP8X4),
                         lhsT_scale=w_scale_bytes[:, a, tiles[c]],
                         rhs=x_codes[a][:, points].bitcast(FP8X4),
                         rhs_scale=x_scale_bytes[a][:, points],

@@ -70,7 +70,7 @@ def tile_picked_grid_lin_bias_sub_l_kernel(tc, xT, w_words, w_scales, b, offs, o
 
         load_tables(0, 4)
         nc.sync.dma_start(offsets[:], offs)
-        for r in range(SCALE_ROWS - 1):
+        for r in range(SCALE_ROWS):
             load_scale_rows(r)
         nc.sync.dma_start(
             bias_rows[0:P:BIAS_STEP, :],
@@ -78,7 +78,6 @@ def tile_picked_grid_lin_bias_sub_l_kernel(tc, xT, w_words, w_scales, b, offs, o
         )
         nc.vector.transpose(bias[:], bias_rows[:])
         load_tables(4, 3)
-        load_scale_rows(SCALE_ROWS - 1)
         load_tables(7, 1)
         load_codes(0, 0, 1, "reused")
         load_codes(0, 1, 1, "w_codes01")
@@ -120,8 +119,8 @@ def tile_picked_grid_lin_bias_sub_l_kernel(tc, xT, w_words, w_scales, b, offs, o
 
         sums = [[psum.tile([P, HALF], F32, name="sums%d_%d" % (c, h)) for h in range(2)] for c in range(M_TILES)]
         for a in range(PASSES):
-            for c in range(M_TILES):
-                for h, points in enumerate(halves):
+            for h, points in enumerate(halves):
+                for c in range(M_TILES):
                     nc.tensor.matmul_mx(
                         out=sums[c][h][:],
                         lhsT=w_codes[a, c].bitcast(FP8X4),

@@ -39,11 +39,12 @@ def tile_picked_grid_lin_bias_sub_l_kernel(tc, xT, w_words, w_scales, b, offs, o
 
         offsets = keep.tile([P, D * LIST_COLS], U16, name="offsets", align_bytes=DMA_ALIGN)
         w_codes = {}
+        loaded_scales = keep.tile([P, PASSES, N], U8, name="loaded_scales", align_bytes=DMA_ALIGN)
         w_scale_bytes = keep.tile([P, PASSES, N], U8, name="w_scale_bytes", align_bytes=DMA_ALIGN)
         bias_rows = keep.tile([P, QUADRANT], F32, name="bias_rows", tag="reused", align_bytes=DMA_ALIGN)
         bias = keep.tile([P, QUADRANT], F32, name="bias", align_bytes=MX_ALIGN)
         nc.vector.memset(bias_rows[:], 0.0)
-        nc.vector.memset(w_scale_bytes[:].rearrange("p a m -> p (a m)").bitcast(I32), 0)
+        nc.vector.memset(loaded_scales[:].rearrange("p a m -> p (a m)").bitcast(I32), 0)
 
         halves = [slice(h * HALF, (h + 1) * HALF) for h in range(2)]
         tiles = [slice(c * P, (c + 1) * P) for c in range(M_TILES)]
@@ -60,7 +61,7 @@ def tile_picked_grid_lin_bias_sub_l_kernel(tc, xT, w_words, w_scales, b, offs, o
                 windows[first + j] = tables[:, j * T : (j + 1) * T]
 
         def load_scale_rows(r):
-            nc.sync.dma_start(w_scale_bytes[r:P:QUADRANT, :, :].bitcast(I32), scale_rows[r].bitcast(I32))
+            nc.sync.dma_start(loaded_scales[r:P:QUADRANT, :, :].bitcast(I32), scale_rows[r].bitcast(I32))
 
         def load_codes(a, first, count, tag):
             codes = keep.tile([P, count * P], U32, name=tag, tag=tag, align_bytes=DMA_ALIGN)
@@ -77,6 +78,10 @@ def tile_picked_grid_lin_bias_sub_l_kernel(tc, xT, w_words, w_scales, b, offs, o
             b.rearrange("(c q j) o -> q c (j o)", c=M_TILES, j=QUADRANT),
         )
         nc.vector.transpose(bias[:], bias_rows[:])
+        nc.vector.tensor_copy(
+            w_scale_bytes[:].rearrange("p a m -> p (a m)").bitcast(I32),
+            loaded_scales[:].rearrange("p a m -> p (a m)").bitcast(I32),
+        )
         load_tables(4, 3)
         load_tables(7, 1)
         load_codes(0, 0, 1, "reused")

@@ -39,7 +39,7 @@ def tile_picked_grid_lin_bias_sub_l_kernel(tc, xT, w_words, w_scales, b, offs, o
 
         offsets = keep.tile([P, D * LIST_COLS], U16, name="offsets", align_bytes=DMA_ALIGN)
         w_codes = {}
-        loaded_scales = keep.tile([P, PASSES, N], U8, name="loaded_scales", align_bytes=DMA_ALIGN)
+        loaded_scales = keep.tile([P, PASSES, N], U8, name="loaded_scales", tag="staged", align_bytes=DMA_ALIGN)
         w_scale_bytes = keep.tile([P, PASSES, N], U8, name="w_scale_bytes", align_bytes=DMA_ALIGN)
         bias_rows = keep.tile([P, QUADRANT], F32, name="bias_rows", tag="reused", align_bytes=DMA_ALIGN)
         bias = keep.tile([P, QUADRANT], F32, name="bias", align_bytes=MX_ALIGN)
@@ -64,7 +64,7 @@ def tile_picked_grid_lin_bias_sub_l_kernel(tc, xT, w_words, w_scales, b, offs, o
             nc.sync.dma_start(loaded_scales[r:P:QUADRANT, :, :].bitcast(I32), scale_rows[r].bitcast(I32))
 
         def load_codes(a, first, count, tag):
-            codes = keep.tile([P, count * P], U32, name=tag, tag=tag, align_bytes=DMA_ALIGN)
+            codes = keep.tile([P, count * P], U32, name="w_codes%d" % a, tag=tag, align_bytes=DMA_ALIGN)
             nc.sync.dma_start(codes[:].bitcast(I32), words[:, a, first * P : (first + count) * P])
             for j in range(count):
                 w_codes[a, first + j] = codes[:, j * P : (j + 1) * P]
@@ -84,9 +84,8 @@ def tile_picked_grid_lin_bias_sub_l_kernel(tc, xT, w_words, w_scales, b, offs, o
         )
         load_tables(4, 3)
         load_tables(7, 1)
-        load_codes(0, 0, 1, "reused")
-        load_codes(0, 1, 1, "w_codes01")
-        load_codes(1, 0, M_TILES, "w_codes1")
+        load_codes(0, 0, M_TILES, "reused")
+        load_codes(1, 0, M_TILES, "staged")
 
         def piece(level):
             return offsets[:, level * LIST_COLS : (level + 1) * LIST_COLS]
@@ -136,12 +135,8 @@ def tile_picked_grid_lin_bias_sub_l_kernel(tc, xT, w_words, w_scales, b, offs, o
                         stop=a == PASSES - 1,
                     )
 
-        for c in range(M_TILES):
-            result = keep.tile([P, V], F32, name="result%d" % c, align_bytes=DMA_ALIGN)
-            column = bias[:, c * BIAS_STEP : c * BIAS_STEP + 1]
-            for h, points in enumerate(halves):
-                nc.vector.tensor_scalar_add(result[:, points], sums[c][h][:], column)
-                if c == 0:
-                    nc.sync.dma_start(out[tiles[c], points], result[:, points])
-            if c > 0:
-                nc.sync.dma_start(out[tiles[c], :], result[:])
+        for h, points in enumerate(halves):
+            for c in range(M_TILES):
+                result = keep.tile([P, HALF], F32, name="result%d_%d" % (c, h), align_bytes=DMA_ALIGN)
+                nc.vector.tensor_scalar_add(result[:], sums[c][h][:], bias[:, c * BIAS_STEP : c * BIAS_STEP + 1])
+                nc.sync.dma_start(out[tiles[c], points], result[:])

@@ -110,7 +110,7 @@ def tile_picked_grid_lin_bias_sub_l_kernel(tc, xT, w_words, w_scales, b, offs, o
                         nc.vector.tensor_copy(quarter, looked_up)
                     else:
                         nc.scalar.activation(quarter, looked_up, COPY)
-                for points in halves:
+                for points in (slice(0, QUARTER), slice(QUARTER, HALF), halves[1]):
                     nc.vector.tensor_copy(grouped[:, points, 3], plain[:, points])
             x_codes.append(keep.tile([P, V], U32, name="x_codes%d" % a, align_bytes=MX_ALIGN))
             x_scale_bytes.append(keep.tile([P, V], U8, name="x_scale_bytes%d" % a, align_bytes=MX_ALIGN))

@@ -64,7 +64,7 @@ def tile_picked_grid_lin_bias_sub_l_kernel(tc, xT, w_words, w_scales, b, offs, o
             nc.sync.dma_start(loaded_scales[r:P:QUADRANT, :, :].bitcast(I32), scale_rows[r].bitcast(I32))
 
         def load_codes(a, first, count, tag):
-            codes = keep.tile([P, count * P], U32, name="w_codes%d" % a, tag=tag, align_bytes=DMA_ALIGN)
+            codes = keep.tile([P, count * P], U32, name="w_codes%d_%d" % (a, first), tag=tag, align_bytes=DMA_ALIGN)
             nc.sync.dma_start(codes[:].bitcast(I32), words[:, a, first * P : (first + count) * P])
             for j in range(count):
                 w_codes[a, first + j] = codes[:, j * P : (j + 1) * P]
@@ -84,7 +84,8 @@ def tile_picked_grid_lin_bias_sub_l_kernel(tc, xT, w_words, w_scales, b, offs, o
         )
         load_tables(4, 3)
         load_tables(7, 1)
-        load_codes(0, 0, M_TILES, "reused")
+        load_codes(0, 0, 1, "reused")
+        load_codes(0, 1, 1, "w_codes0_1")
         load_codes(1, 0, M_TILES, "staged")
 
         def piece(level):
@@ -136,7 +137,10 @@ def tile_picked_grid_lin_bias_sub_l_kernel(tc, xT, w_words, w_scales, b, offs, o
                     )
 
         for h, points in enumerate(halves):
+            result = keep.tile([P, M_TILES, HALF], F32, name="result%d" % h, align_bytes=DMA_ALIGN)
             for c in range(M_TILES):
-                result = keep.tile([P, HALF], F32, name="result%d_%d" % (c, h), align_bytes=DMA_ALIGN)
-                nc.vector.tensor_scalar_add(result[:], sums[c][h][:], bias[:, c * BIAS_STEP : c * BIAS_STEP + 1])
-                nc.sync.dma_start(out[tiles[c], points], result[:])
+                nc.vector.tensor_scalar_add(result[:, c, :], sums[c][h][:], bias[:, c * BIAS_STEP : c * BIAS_STEP + 1])
+                if h == 0:
+                    nc.sync.dma_start(out[tiles[c], points], result[:, c, :])
+            if h > 0:
+                nc.sync.dma_start(out.rearrange("(c p) v -> p c v", p=P)[:, :, points], result[:])

@@ -24,6 +24,7 @@ LIST_COLS = V // 16
 HALF = V // 2
 QUARTER = V // 4
 QUARTER_COLS = LIST_COLS // 4
+SCALAR_POINTS = (64, 64)
 QUADRANT = 32
 BIAS_STEP = QUADRANT // M_TILES
 SCALE_ROWS = 4
@@ -94,25 +95,36 @@ def tile_picked_grid_lin_bias_sub_l_kernel(tc, xT, w_words, w_scales, b, offs, o
         x_codes, x_scale_bytes = [], []
         for a in range(PASSES):
             grouped = keep.tile([P, V, PACK], BF16, name="grouped%d" % a, align_bytes=MX_ALIGN)
-            pair = keep.tile([P, 2, V], F32, name="pair%d" % a, align_bytes=MX_ALIGN)
-            for t in range(2):
-                nc.scalar.activation(pair[:, t, :], windows[PACK * a + t].indirect(piece(PACK * a + t)), COPY)
-            nc.vector.tensor_copy(grouped[:, :, 2], windows[PACK * a + 2].indirect(piece(PACK * a + 2)))
-            nc.vector.tensor_copy(grouped[:, :, 0:2], pair[:].rearrange("p t v -> p v t"))
+            planes = keep.tile([P, PACK, V], F32, name="planes%d" % a, align_bytes=MX_ALIGN)
+            by_point = planes[:].rearrange("p t v -> p v t")
             level = PACK * a + 3
+            for t in (0, 1) if level < D - 1 else (1, 2):
+                nc.scalar.activation(planes[:, t, :], windows[PACK * a + t].indirect(piece(PACK * a + t)), COPY)
             if level < D - 1:
+                nc.vector.tensor_copy(grouped[:, :, 2], windows[level - 1].indirect(piece(level - 1)))
+                nc.vector.tensor_copy(grouped[:, :, 0:2], by_point[:, :, 0:2])
                 nc.vector.tensor_copy(grouped[:, :, 3], windows[level].indirect(piece(level)))
             else:
+                nc.vector.tensor_copy(planes[:, 0, :], windows[level - 3].indirect(piece(level - 3)))
                 plain = keep.tile([P, V], BF16, name="plain", align_bytes=MX_ALIGN)
+                cuts = [h.stop - w for h, w in zip(halves, SCALAR_POINTS)]
+                for h, cut in zip(halves, cuts):
+                    nc.vector.tensor_copy(grouped[:, h.start : cut, 0:3], by_point[:, h.start : cut, 0:3])
+                    nc.vector.tensor_copy(grouped[:, cut : h.stop, 0:2], by_point[:, cut : h.stop, 0:2])
                 for q in range(4):
-                    quarter = plain[:, q * QUARTER : (q + 1) * QUARTER]
+                    points = slice(q * QUARTER, (q + 1) * QUARTER)
                     looked_up = windows[level].indirect(piece(level)[:, q * QUARTER_COLS : (q + 1) * QUARTER_COLS])
                     if q % 2 == 0:
-                        nc.vector.tensor_copy(quarter, looked_up)
+                        nc.vector.tensor_copy(plain[:, points], looked_up)
                     else:
-                        nc.scalar.activation(quarter, looked_up, COPY)
-                for points in (slice(0, QUARTER), slice(QUARTER, HALF), halves[1]):
-                    nc.vector.tensor_copy(grouped[:, points, 3], plain[:, points])
+                        nc.scalar.activation(planes[:, 3, points], looked_up, COPY)
+                for h, cut in zip(halves, cuts):
+                    middle = h.start + QUARTER
+                    nc.vector.tensor_copy(grouped[:, h.start : middle, 3], plain[:, h.start : middle])
+                    if cut > middle:
+                        nc.vector.tensor_copy(grouped[:, middle:cut, 3], planes[:, 3, middle:cut])
+                    if cut < h.stop:
+                        nc.scalar.activation(grouped[:, cut : h.stop, 2:4], by_point[:, cut : h.stop, 2:4], COPY)
             x_codes.append(keep.tile([P, V], U32, name="x_codes%d" % a, align_bytes=MX_ALIGN))
             x_scale_bytes.append(keep.tile([P, V], U8, name="x_scale_bytes%d" % a, align_bytes=MX_ALIGN))
             for points in halves:

@@ -48,6 +48,7 @@ def tile_picked_grid_lin_bias_sub_l_kernel(tc, xT, w_words, w_scales, b, offs, o
         nc.vector.memset(loaded_scales[:].rearrange("p a m -> p (a m)").bitcast(I32), 0)
 
         halves = [slice(h * HALF, (h + 1) * HALF) for h in range(2)]
+        quarters = [slice(q * QUARTER, (q + 1) * QUARTER) for q in range(4)]
         tiles = [slice(c * P, (c + 1) * P) for c in range(M_TILES)]
         windows = {}
         words = w_words.rearrange("a p m r -> p a (m r)").bitcast(I32)
@@ -127,7 +128,7 @@ def tile_picked_grid_lin_bias_sub_l_kernel(tc, xT, w_words, w_scales, b, offs, o
                         nc.scalar.activation(grouped[:, cut : h.stop, 2:4], by_point[:, cut : h.stop, 2:4], COPY)
             x_codes.append(keep.tile([P, V], U32, name="x_codes%d" % a, align_bytes=MX_ALIGN))
             x_scale_bytes.append(keep.tile([P, V], U8, name="x_scale_bytes%d" % a, align_bytes=MX_ALIGN))
-            for points in halves:
+            for points in halves if level < D - 1 else quarters:
                 nc.vector.quantize_mx(
                     out=x_codes[a][:, points].bitcast(FP8X4),
                     scales=x_scale_bytes[a][:, points],

@@ -128,7 +128,7 @@ def tile_picked_grid_lin_bias_sub_l_kernel(tc, xT, w_words, w_scales, b, offs, o
                         nc.scalar.activation(grouped[:, cut : h.stop, 2:4], by_point[:, cut : h.stop, 2:4], COPY)
             x_codes.append(keep.tile([P, V], U32, name="x_codes%d" % a, align_bytes=MX_ALIGN))
             x_scale_bytes.append(keep.tile([P, V], U8, name="x_scale_bytes%d" % a, align_bytes=MX_ALIGN))
-            for points in halves if level < D - 1 else quarters:
+            for points in halves if level < D - 1 else (quarters[0], quarters[1], halves[1]):
                 nc.vector.quantize_mx(
                     out=x_codes[a][:, points].bitcast(FP8X4),
                     scales=x_scale_bytes[a][:, points],

@@ -24,7 +24,6 @@ LIST_COLS = V // 16
 HALF = V // 2
 QUARTER = V // 4
 QUARTER_COLS = LIST_COLS // 4
-SCALAR_POINTS = (64, 64)
 QUADRANT = 32
 BIAS_STEP = QUADRANT // M_TILES
 SCALE_ROWS = 4
@@ -108,24 +107,20 @@ def tile_picked_grid_lin_bias_sub_l_kernel(tc, xT, w_words, w_scales, b, offs, o
             else:
                 nc.vector.tensor_copy(planes[:, 0, :], windows[level - 3].indirect(piece(level - 3)))
                 plain = keep.tile([P, V], BF16, name="plain", align_bytes=MX_ALIGN)
-                cuts = [h.stop - w for h, w in zip(halves, SCALAR_POINTS)]
-                for h, cut in zip(halves, cuts):
-                    nc.vector.tensor_copy(grouped[:, h.start : cut, 0:3], by_point[:, h.start : cut, 0:3])
-                    nc.vector.tensor_copy(grouped[:, cut : h.stop, 0:2], by_point[:, cut : h.stop, 0:2])
-                for q in range(4):
-                    points = slice(q * QUARTER, (q + 1) * QUARTER)
+                last_two = keep.tile([P, 2, QUARTER], BF16, name="last_two", align_bytes=MX_ALIGN)
+                nc.scalar.activation(last_two[:, 0, :], planes[:, 2, quarters[2]], COPY)
+                nc.vector.tensor_copy(grouped[:, halves[0], 0:3], by_point[:, halves[0], 0:3])
+                nc.vector.tensor_copy(grouped[:, quarters[2], 0:2], by_point[:, quarters[2], 0:2])
+                nc.vector.tensor_copy(grouped[:, quarters[3], 0:3], by_point[:, quarters[3], 0:3])
+                for q, points in enumerate(quarters):
                     looked_up = windows[level].indirect(piece(level)[:, q * QUARTER_COLS : (q + 1) * QUARTER_COLS])
                     if q % 2 == 0:
-                        nc.vector.tensor_copy(plain[:, points], looked_up)
+                        nc.vector.tensor_copy(last_two[:, 1, :] if q == 2 else plain[:, points], looked_up)
                     else:
-                        nc.scalar.activation(planes[:, 3, points], looked_up, COPY)
-                for h, cut in zip(halves, cuts):
-                    middle = h.start + QUARTER
-                    nc.vector.tensor_copy(grouped[:, h.start : middle, 3], plain[:, h.start : middle])
-                    if cut > middle:
-                        nc.vector.tensor_copy(grouped[:, middle:cut, 3], planes[:, 3, middle:cut])
-                    if cut < h.stop:
-                        nc.scalar.activation(grouped[:, cut : h.stop, 2:4], by_point[:, cut : h.stop, 2:4], COPY)
+                        nc.scalar.activation(plain[:, points], looked_up, COPY)
+                for q in (0, 1, 3):
+                    nc.vector.tensor_copy(grouped[:, quarters[q], 3], plain[:, quarters[q]])
+                nc.scalar.copy(grouped[:, quarters[2], 2:4], last_two[:].rearrange("p t v -> p v t"))
             x_codes.append(keep.tile([P, V], U32, name="x_codes%d" % a, align_bytes=MX_ALIGN))
             x_scale_bytes.append(keep.tile([P, V], U8, name="x_scale_bytes%d" % a, align_bytes=MX_ALIGN))
             for points in halves if level < D - 1 else (quarters[0], quarters[1], halves[1]):

@@ -23,7 +23,6 @@ M_TILES = N // P
 LIST_COLS = V // 16
 HALF = V // 2
 QUARTER = V // 4
-QUARTER_COLS = LIST_COLS // 4
 QUADRANT = 32
 BIAS_STEP = QUADRANT // M_TILES
 SCALE_ROWS = 4
@@ -83,52 +82,51 @@ def tile_picked_grid_lin_bias_sub_l_kernel(tc, xT, w_words, w_scales, b, offs, o
             w_scale_bytes[:].rearrange("p a m -> p (a m)").bitcast(I32),
             loaded_scales[:].rearrange("p a m -> p (a m)").bitcast(I32),
         )
-        load_tables(4, 3)
+        load_tables(4, 2)
+        load_tables(6, 1)
         load_tables(7, 1)
-        load_codes(0, 0, 1, "reused")
-        load_codes(0, 1, 1, "w_codes0_1")
+        load_codes(0, 0, M_TILES, "reused")
         load_codes(1, 0, M_TILES, "staged")
 
-        def piece(level):
-            return offsets[:, level * LIST_COLS : (level + 1) * LIST_COLS]
+        def looked_up(level, points):
+            first = level * LIST_COLS
+            return windows[level].indirect(offsets[:, first + points.start // 16 : first + points.stop // 16])
 
-        x_codes, x_scale_bytes = [], []
+        def quantise(a, points):
+            nc.vector.quantize_mx(
+                out=x_codes[a][:, points].bitcast(FP8X4),
+                scales=x_scale_bytes[a][:, points],
+                in_=grouped[a][:, points, :].rearrange("p v t -> p (v t)"),
+            )
+
+        every = slice(0, V)
+        grouped = [keep.tile([P, V, PACK], BF16, name="grouped%d" % a, align_bytes=MX_ALIGN) for a in range(PASSES)]
+        x_codes = [keep.tile([P, V], U32, name="x_codes%d" % a, align_bytes=MX_ALIGN) for a in range(PASSES)]
+        x_scale_bytes = [keep.tile([P, V], U8, name="x_scale_bytes%d" % a, align_bytes=MX_ALIGN) for a in range(PASSES)]
+
         for a in range(PASSES):
-            grouped = keep.tile([P, V, PACK], BF16, name="grouped%d" % a, align_bytes=MX_ALIGN)
-            planes = keep.tile([P, PACK, V], F32, name="planes%d" % a, align_bytes=MX_ALIGN)
-            by_point = planes[:].rearrange("p t v -> p v t")
-            level = PACK * a + 3
-            for t in (0, 1) if level < D - 1 else (1, 2):
-                nc.scalar.activation(planes[:, t, :], windows[PACK * a + t].indirect(piece(PACK * a + t)), COPY)
-            if level < D - 1:
-                nc.vector.tensor_copy(grouped[:, :, 2], windows[level - 1].indirect(piece(level - 1)))
-                nc.vector.tensor_copy(grouped[:, :, 0:2], by_point[:, :, 0:2])
-                nc.vector.tensor_copy(grouped[:, :, 3], windows[level].indirect(piece(level)))
-            else:
-                nc.vector.tensor_copy(planes[:, 0, :], windows[level - 3].indirect(piece(level - 3)))
-                plain = keep.tile([P, V], BF16, name="plain", align_bytes=MX_ALIGN)
-                last_two = keep.tile([P, 2, QUARTER], BF16, name="last_two", align_bytes=MX_ALIGN)
-                nc.scalar.activation(last_two[:, 0, :], planes[:, 2, quarters[2]], COPY)
-                nc.vector.tensor_copy(grouped[:, halves[0], 0:3], by_point[:, halves[0], 0:3])
-                nc.vector.tensor_copy(grouped[:, quarters[2], 0:2], by_point[:, quarters[2], 0:2])
-                nc.vector.tensor_copy(grouped[:, quarters[3], 0:3], by_point[:, quarters[3], 0:3])
-                for q, points in enumerate(quarters):
-                    looked_up = windows[level].indirect(piece(level)[:, q * QUARTER_COLS : (q + 1) * QUARTER_COLS])
-                    if q % 2 == 0:
-                        nc.vector.tensor_copy(last_two[:, 1, :] if q == 2 else plain[:, points], looked_up)
-                    else:
-                        nc.scalar.activation(plain[:, points], looked_up, COPY)
-                for q in (0, 1, 3):
-                    nc.vector.tensor_copy(grouped[:, quarters[q], 3], plain[:, quarters[q]])
-                nc.scalar.copy(grouped[:, quarters[2], 2:4], last_two[:].rearrange("p t v -> p v t"))
-            x_codes.append(keep.tile([P, V], U32, name="x_codes%d" % a, align_bytes=MX_ALIGN))
-            x_scale_bytes.append(keep.tile([P, V], U8, name="x_scale_bytes%d" % a, align_bytes=MX_ALIGN))
-            for points in halves if level < D - 1 else (quarters[0], quarters[1], halves[1]):
-                nc.vector.quantize_mx(
-                    out=x_codes[a][:, points].bitcast(FP8X4),
-                    scales=x_scale_bytes[a][:, points],
-                    in_=grouped[:, points, :].rearrange("p v t -> p (v t)"),
-                )
+            planes = keep.tile([P, 2, V], F32, name="planes%d" % a, align_bytes=MX_ALIGN)
+            for t in range(2):
+                nc.scalar.activation(planes[:, t, :], looked_up(PACK * a + t, every), COPY)
+            nc.vector.tensor_copy(grouped[a][:, :, 0:2], planes[:].rearrange("p t v -> p v t"))
+            if a == 0:
+                for t in (2, 3):
+                    nc.vector.tensor_copy(grouped[a][:, :, t], looked_up(t, every))
+                quantise(a, every)
+
+        plain = keep.tile([P, 2, HALF], BF16, name="plain", align_bytes=MX_ALIGN)
+        nc.scalar.activation(grouped[1][:, halves[0], 2], looked_up(D - 2, halves[0]), COPY)
+        nc.vector.tensor_copy(plain[:, 0, :], looked_up(D - 2, halves[1]))
+        nc.vector.tensor_copy(grouped[1][:, halves[1], 2], plain[:, 0, :])
+        for q in range(2):
+            nc.scalar.activation(grouped[1][:, quarters[q], 3], looked_up(D - 1, quarters[q]), COPY)
+        for q in range(2):
+            nc.vector.tensor_copy(plain[:, 1, quarters[q]], looked_up(D - 1, quarters[2 + q]))
+        nc.vector.tensor_copy(grouped[1][:, quarters[2], 3], plain[:, 1, quarters[0]])
+        quantise(1, quarters[0])
+        nc.vector.tensor_copy(grouped[1][:, quarters[3], 3], plain[:, 1, quarters[1]])
+        quantise(1, quarters[1])
+        quantise(1, halves[1])
 
         sums = [[psum.tile([P, HALF], F32, name="sums%d_%d" % (c, h)) for h in range(2)] for c in range(M_TILES)]
         for a in range(PASSES):

@@ -82,10 +82,10 @@ def tile_picked_grid_lin_bias_sub_l_kernel(tc, xT, w_words, w_scales, b, offs, o
             w_scale_bytes[:].rearrange("p a m -> p (a m)").bitcast(I32),
             loaded_scales[:].rearrange("p a m -> p (a m)").bitcast(I32),
         )
-        load_tables(4, 2)
-        load_tables(6, 1)
+        load_tables(4, 3)
         load_tables(7, 1)
-        load_codes(0, 0, M_TILES, "reused")
+        load_codes(0, 0, 1, "reused")
+        load_codes(0, 1, 1, "w_codes0_1")
         load_codes(1, 0, M_TILES, "staged")
 
         def looked_up(level, points):
@@ -104,27 +104,30 @@ def tile_picked_grid_lin_bias_sub_l_kernel(tc, xT, w_words, w_scales, b, offs, o
         x_codes = [keep.tile([P, V], U32, name="x_codes%d" % a, align_bytes=MX_ALIGN) for a in range(PASSES)]
         x_scale_bytes = [keep.tile([P, V], U8, name="x_scale_bytes%d" % a, align_bytes=MX_ALIGN) for a in range(PASSES)]
 
-        for a in range(PASSES):
-            planes = keep.tile([P, 2, V], F32, name="planes%d" % a, align_bytes=MX_ALIGN)
-            for t in range(2):
-                nc.scalar.activation(planes[:, t, :], looked_up(PACK * a + t, every), COPY)
-            nc.vector.tensor_copy(grouped[a][:, :, 0:2], planes[:].rearrange("p t v -> p v t"))
-            if a == 0:
-                for t in (2, 3):
-                    nc.vector.tensor_copy(grouped[a][:, :, t], looked_up(t, every))
-                quantise(a, every)
+        planes = keep.tile([P, 2, V], F32, name="planes0", align_bytes=MX_ALIGN)
+        for t in range(2):
+            nc.scalar.activation(planes[:, t, :], looked_up(t, every), COPY)
+        nc.vector.tensor_copy(grouped[0][:, :, 2], looked_up(2, every))
+        nc.vector.tensor_copy(grouped[0][:, :, 0:2], planes[:].rearrange("p t v -> p v t"))
+        nc.vector.tensor_copy(grouped[0][:, :, 3], looked_up(3, every))
+        quantise(0, every)
 
-        plain = keep.tile([P, 2, HALF], BF16, name="plain", align_bytes=MX_ALIGN)
-        nc.scalar.activation(grouped[1][:, halves[0], 2], looked_up(D - 2, halves[0]), COPY)
-        nc.vector.tensor_copy(plain[:, 0, :], looked_up(D - 2, halves[1]))
-        nc.vector.tensor_copy(grouped[1][:, halves[1], 2], plain[:, 0, :])
+        planes = keep.tile([P, 2, V], F32, name="planes1", align_bytes=MX_ALIGN)
+        third = keep.tile([P, V], F32, name="third", align_bytes=MX_ALIGN)
+        for t in range(2):
+            nc.scalar.activation(planes[:, t, :], looked_up(PACK + t, every), COPY)
+        nc.vector.tensor_copy(third[:], looked_up(D - 2, every))
+        nc.scalar.activation(grouped[1][:, halves[0], 2], third[:, halves[0]], COPY)
+        nc.vector.tensor_copy(grouped[1][:, halves[1], 2], third[:, halves[1]])
+        nc.vector.tensor_copy(grouped[1][:, :, 0:2], planes[:].rearrange("p t v -> p v t"))
+        plain = keep.tile([P, HALF], BF16, name="plain", align_bytes=MX_ALIGN)
         for q in range(2):
             nc.scalar.activation(grouped[1][:, quarters[q], 3], looked_up(D - 1, quarters[q]), COPY)
         for q in range(2):
-            nc.vector.tensor_copy(plain[:, 1, quarters[q]], looked_up(D - 1, quarters[2 + q]))
-        nc.vector.tensor_copy(grouped[1][:, quarters[2], 3], plain[:, 1, quarters[0]])
+            nc.vector.tensor_copy(plain[:, quarters[q]], looked_up(D - 1, quarters[2 + q]))
+        nc.vector.tensor_copy(grouped[1][:, quarters[2], 3], plain[:, quarters[0]])
         quantise(1, quarters[0])
-        nc.vector.tensor_copy(grouped[1][:, quarters[3], 3], plain[:, 1, quarters[1]])
+        nc.vector.tensor_copy(grouped[1][:, quarters[3], 3], plain[:, quarters[1]])
         quantise(1, quarters[1])
         quantise(1, halves[1])
 

@@ -114,22 +114,20 @@ def tile_picked_grid_lin_bias_sub_l_kernel(tc, xT, w_words, w_scales, b, offs, o
 
         planes = keep.tile([P, 2, V], F32, name="planes1", align_bytes=MX_ALIGN)
         third = keep.tile([P, V], F32, name="third", align_bytes=MX_ALIGN)
-        for t in range(2):
-            nc.scalar.activation(planes[:, t, :], looked_up(PACK + t, every), COPY)
+        direct = slice(0, 3 * QUARTER)
         nc.vector.tensor_copy(third[:], looked_up(D - 2, every))
-        nc.scalar.activation(grouped[1][:, halves[0], 2], third[:, halves[0]], COPY)
-        nc.vector.tensor_copy(grouped[1][:, halves[1], 2], third[:, halves[1]])
+        nc.scalar.activation(planes[:, 0, :], looked_up(PACK, every), COPY)
+        nc.vector.tensor_copy(planes[:, 1, :], looked_up(PACK + 1, every))
+        nc.scalar.activation(grouped[1][:, direct, 2], third[:, direct], COPY)
+        nc.vector.tensor_copy(grouped[1][:, quarters[3], 2], third[:, quarters[3]])
         nc.vector.tensor_copy(grouped[1][:, :, 0:2], planes[:].rearrange("p t v -> p v t"))
-        plain = keep.tile([P, HALF], BF16, name="plain", align_bytes=MX_ALIGN)
-        for q in range(2):
+        plain = keep.tile([P, QUARTER], BF16, name="plain", align_bytes=MX_ALIGN)
+        for q in range(3):
             nc.scalar.activation(grouped[1][:, quarters[q], 3], looked_up(D - 1, quarters[q]), COPY)
-        for q in range(2):
-            nc.vector.tensor_copy(plain[:, quarters[q]], looked_up(D - 1, quarters[2 + q]))
-        nc.vector.tensor_copy(grouped[1][:, quarters[2], 3], plain[:, quarters[0]])
-        quantise(1, quarters[0])
-        nc.vector.tensor_copy(grouped[1][:, quarters[3], 3], plain[:, quarters[1]])
-        quantise(1, quarters[1])
-        quantise(1, halves[1])
+        nc.vector.tensor_copy(plain[:], looked_up(D - 1, quarters[3]))
+        nc.vector.tensor_copy(grouped[1][:, quarters[3], 3], plain[:])
+        for q in (0, 1, 3, 2):
+            quantise(1, quarters[q])
 
         sums = [[psum.tile([P, HALF], F32, name="sums%d_%d" % (c, h)) for h in range(2)] for c in range(M_TILES)]
         for a in range(PASSES):

from contextlib import ExitStack

import concourse.mybir as mybir

K, T, D, V, N = 1024, 2048, 8, 256, 256
FLOPS = 2 * K * V * N

F32 = mybir.dt.float32
BF16 = mybir.dt.bfloat16
I32 = mybir.dt.int32
U32 = mybir.dt.uint32
U16 = mybir.dt.uint16
U8 = mybir.dt.uint8
FP8X4 = mybir.dt.float8_e4m3fn_x4

COPY = mybir.ActivationFunctionType.Copy

P = 128
PACK = 4
K_PASS = P * PACK
PASSES = K // K_PASS
M_TILES = N // P
LIST_COLS = V // 16
HALF = V // 2
QUARTER = V // 4
QUADRANT = 32
BIAS_STEP = QUADRANT // M_TILES
SCALE_ROWS = 4
MX_ALIGN = 64
DMA_ALIGN = 256


def tile_picked_grid_lin_bias_sub_l_kernel(tc, xT, w_words, w_scales, b, offs, out):
    nc = tc.nc
    with ExitStack() as ctx:
        keep = ctx.enter_context(tc.tile_pool(name="keep", bufs=1))
        psum = ctx.enter_context(tc.psum_pool(name="psum", bufs=1))

        offsets = keep.tile([P, D * LIST_COLS], U16, name="offsets", align_bytes=DMA_ALIGN)
        w_codes = {}
        loaded_scales = keep.tile([P, PASSES, N], U8, name="loaded_scales", tag="staged", align_bytes=DMA_ALIGN)
        w_scale_bytes = keep.tile([P, PASSES, N], U8, name="w_scale_bytes", align_bytes=DMA_ALIGN)
        bias_rows = keep.tile([P, QUADRANT], F32, name="bias_rows", tag="reused", align_bytes=DMA_ALIGN)
        bias = keep.tile([P, QUADRANT], F32, name="bias", align_bytes=MX_ALIGN)
        nc.vector.memset(bias_rows[:], 0.0)
        nc.vector.memset(loaded_scales[:].rearrange("p a m -> p (a m)").bitcast(I32), 0)

        halves = [slice(h * HALF, (h + 1) * HALF) for h in range(2)]
        quarters = [slice(q * QUARTER, (q + 1) * QUARTER) for q in range(4)]
        tiles = [slice(c * P, (c + 1) * P) for c in range(M_TILES)]
        windows = {}
        words = w_words.rearrange("a p m r -> p a (m r)").bitcast(I32)
        scale_rows = w_scales.rearrange("a (q r) m -> r q a m", r=SCALE_ROWS)

        def load_tables(first, count):
            a, t = divmod(first, PACK)
            rows = xT[a * K_PASS : (a + 1) * K_PASS, :].rearrange("(p t) c -> p (t c)", t=PACK)
            tables = keep.tile([P, count * T], F32, name="tables%d" % first, align_bytes=DMA_ALIGN)
            nc.sync.dma_start(tables[:], rows[:, t * T : (t + count) * T])
            for j in range(count):
                windows[first + j] = tables[:, j * T : (j + 1) * T]

        def load_scale_rows(r):
            nc.sync.dma_start(loaded_scales[r:P:QUADRANT, :, :].bitcast(I32), scale_rows[r].bitcast(I32))

        def load_codes(a, first, count, tag):
            codes = keep.tile([P, count * P], U32, name="w_codes%d_%d" % (a, first), tag=tag, align_bytes=DMA_ALIGN)
            nc.sync.dma_start(codes[:].bitcast(I32), words[:, a, first * P : (first + count) * P])
            for j in range(count):
                w_codes[a, first + j] = codes[:, j * P : (j + 1) * P]

        load_tables(0, 4)
        nc.sync.dma_start(offsets[:], offs)
        for r in range(SCALE_ROWS):
            load_scale_rows(r)
        nc.sync.dma_start(
            bias_rows[0:P:BIAS_STEP, :],
            b.rearrange("(c q j) o -> q c (j o)", c=M_TILES, j=QUADRANT),
        )
        nc.vector.transpose(bias[:], bias_rows[:])
        nc.vector.tensor_copy(
            w_scale_bytes[:].rearrange("p a m -> p (a m)").bitcast(I32),
            loaded_scales[:].rearrange("p a m -> p (a m)").bitcast(I32),
        )
        load_tables(4, 3)
        load_tables(7, 1)
        load_codes(0, 0, 1, "reused")
        load_codes(0, 1, 1, "w_codes0_1")
        load_codes(1, 0, M_TILES, "staged")

        def looked_up(level, points):
            first = level * LIST_COLS
            return windows[level].indirect(offsets[:, first + points.start // 16 : first + points.stop // 16])

        def quantise(a, points):
            nc.vector.quantize_mx(
                out=x_codes[a][:, points].bitcast(FP8X4),
                scales=x_scale_bytes[a][:, points],
                in_=grouped[a][:, points, :].rearrange("p v t -> p (v t)"),
            )

        every = slice(0, V)
        grouped = [keep.tile([P, V, PACK], BF16, name="grouped%d" % a, align_bytes=MX_ALIGN) for a in range(PASSES)]
        x_codes = [keep.tile([P, V], U32, name="x_codes%d" % a, align_bytes=MX_ALIGN) for a in range(PASSES)]
        x_scale_bytes = [keep.tile([P, V], U8, name="x_scale_bytes%d" % a, align_bytes=MX_ALIGN) for a in range(PASSES)]

        planes = keep.tile([P, 2, V], F32, name="planes0", align_bytes=MX_ALIGN)
        for t in range(2):
            nc.scalar.activation(planes[:, t, :], looked_up(t, every), COPY)
        nc.vector.tensor_copy(grouped[0][:, :, 2], looked_up(2, every))
        nc.vector.tensor_copy(grouped[0][:, :, 0:2], planes[:].rearrange("p t v -> p v t"))
        nc.vector.tensor_copy(grouped[0][:, :, 3], looked_up(3, every))
        quantise(0, every)

        planes = keep.tile([P, 2, V], F32, name="planes1", align_bytes=MX_ALIGN)
        third = keep.tile([P, V], F32, name="third", align_bytes=MX_ALIGN)
        direct = slice(0, 3 * QUARTER)
        nc.vector.tensor_copy(third[:], looked_up(D - 2, every))
        nc.scalar.activation(planes[:, 0, :], looked_up(PACK, every), COPY)
        nc.vector.tensor_copy(planes[:, 1, :], looked_up(PACK + 1, every))
        nc.scalar.activation(grouped[1][:, direct, 2], third[:, direct], COPY)
        nc.vector.tensor_copy(grouped[1][:, quarters[3], 2], third[:, quarters[3]])
        nc.vector.tensor_copy(grouped[1][:, :, 0:2], planes[:].rearrange("p t v -> p v t"))
        plain = keep.tile([P, QUARTER], BF16, name="plain", align_bytes=MX_ALIGN)
        for q in range(3):
            nc.scalar.activation(grouped[1][:, quarters[q], 3], looked_up(D - 1, quarters[q]), COPY)
        nc.vector.tensor_copy(plain[:], looked_up(D - 1, quarters[3]))
        nc.vector.tensor_copy(grouped[1][:, quarters[3], 3], plain[:])
        for q in (0, 1, 3, 2):
            quantise(1, quarters[q])

        sums = [[psum.tile([P, HALF], F32, name="sums%d_%d" % (c, h)) for h in range(2)] for c in range(M_TILES)]
        for a in range(PASSES):
            for h, points in enumerate(halves):
                for c in range(M_TILES):
                    nc.tensor.matmul_mx(
                        out=sums[c][h][:],
                        lhsT=w_codes[a, c].bitcast(FP8X4),
                        lhsT_scale=w_scale_bytes[:, a, tiles[c]],
                        rhs=x_codes[a][:, points].bitcast(FP8X4),
                        rhs_scale=x_scale_bytes[a][:, points],
                        start=a == 0,
                        stop=a == PASSES - 1,
                    )

        for h, points in enumerate(halves):
            result = keep.tile([P, M_TILES, HALF], F32, name="result%d" % h, align_bytes=DMA_ALIGN)
            for c in range(M_TILES):
                nc.vector.tensor_scalar_add(result[:, c, :], sums[c][h][:], bias[:, c * BIAS_STEP : c * BIAS_STEP + 1])
                if h == 0:
                    nc.sync.dma_start(out[tiles[c], points], result[:, c, :])
            if h > 0:
                nc.sync.dma_start(out.rearrange("(c p) v -> p c v", p=P)[:, :, points], result[:])
